import numpy as np
import ml_dtypes


def mxq(x, axis, fmt="e4m3"):
    dtype, down = {"e4m3": (ml_dtypes.float8_e4m3fn, 7), "e5m2": (ml_dtypes.float8_e5m2, 14)}[fmt]
    v = np.moveaxis(np.asarray(x, np.float32).astype(ml_dtypes.bfloat16).astype(np.float64), axis, -1)
    blocks = v.reshape(v.shape[:-1] + (-1, 32))
    amax = np.abs(blocks).max(-1, keepdims=True)
    byte = np.maximum(np.where(amax > 0, np.frexp(amax)[1] - 1 + 127, 0) - down, 1)
    scale = np.exp2(byte - 127.0)
    codes = (blocks / scale).astype(np.float32).astype(dtype).astype(np.float64)
    return np.moveaxis((codes * scale).reshape(v.shape), -1, axis)


WIDE = False


def mx_kscale(k):
    if not WIDE:
        return np.ones(k)
    levels = np.array([30, -30])
    if k % 512:
        return np.exp2(np.random.permutation(np.resize(levels, k // 32))).repeat(32)
    a = np.empty((k // 512, 16))
    for p in range(k // 512):
        a[p, :8] = np.random.permutation(np.resize(levels, 8))
        for g in range(8):
            far = levels[np.abs(levels - a[p, g]) >= 10]
            a[p, g + 8] = far[np.random.randint(len(far))]
    return np.exp2(a.ravel()).repeat(32)


BF16 = ml_dtypes.bfloat16


def bf(x):
    return np.asarray(x, np.float32).astype(BF16)


def f64(x):
    return np.asarray(x).astype(np.float64)

E4M3FN = np.array([(-1.0 if i & 128 else 1.0) * ((1.0 + (i & 7) / 8.0) * 2.0 ** (((i >> 3) & 15) - 7) if i & 120 else (i & 7) * 2.0 ** -9) for i in range(256)])


def e4m3fn_bytes(y):
    return np.clip(np.asarray(y, np.float64), -448.0, 448.0).astype(np.float32).astype(ml_dtypes.float8_e4m3fn).view(np.uint8)


def e4m3fn_values(b):
    return E4M3FN[b]

def planes(Y):
    n, m = Y.shape
    b = f64(bf(Y)).reshape(n // 32, 32, m)
    amax = np.abs(b).max(1)
    byte = np.clip(np.where(amax > 0, np.frexp(amax)[1] - 1 + 127 - 7, 1), 1, 254)
    codes = (b * np.exp2(127.0 - byte)[:, None, :]).reshape(n, m).astype(np.float32).astype(ml_dtypes.float8_e4m3fn).view(np.uint8)
    words = codes.reshape(n // 512, 128, 4, m).transpose(0, 1, 3, 2)
    return np.ascontiguousarray(words), np.ascontiguousarray(byte.astype(np.uint8).reshape(n // 512, 16, m))


T, K, F, G = 1536, 2048, 1024, 32

DF = 4.0


def setup_inputs():
    s = mx_kscale(K)
    R = np.random.standard_t(DF, size=(T, K)) * s[None, :]
    R_scale = (np.abs(R).reshape(T, K // G, G).max(axis=2) / 448.0).astype(np.float32)
    R_bytes = e4m3fn_bytes(R / np.repeat(f64(R_scale), G, axis=1))
    X = np.random.randn(K, F) / np.sqrt(2.0 * K) / s[:, None]
    inv_c = np.exp(0.3 * np.random.randn(1, F))
    step = 2.0 * np.exp(0.8 * np.random.randn(1, F))
    return {"R_bytes": R_bytes, "R_scale": R_scale, "X": bf(X), "inv_c": bf(inv_c), "step": bf(step)}


def reference(R_bytes, R_scale, X, inv_c, step):
    R = e4m3fn_values(R_bytes) * np.repeat(f64(R_scale), G, axis=1)
    S = mxq(R, 1, "e5m2") @ mxq(f64(X), 0, "e4m3")
    u = S * f64(inv_c)
    w = 1.0 / (1.0 + u * u)
    y = f64(step) * (u * w)
    words, scales = planes(y.T)
    return y, words, scales

@@ -1,0 +1,378 @@
+from contextlib import ExitStack
+
+import concourse.mybir as mybir
+from concourse.masks import make_identity
+
+T, K, F = 1536, 2048, 1024
+FLOPS = 2 * T * K * F
+
+F32 = mybir.dt.float32
+BF16 = mybir.dt.bfloat16
+I32 = mybir.dt.int32
+U32 = mybir.dt.uint32
+U8 = mybir.dt.uint8
+FP8 = mybir.dt.float8_e4m3fn
+E4X4 = mybir.dt.float8_e4m3fn_x4
+E5X4 = mybir.dt.float8_e5m2_x4
+ACT = mybir.ActivationFunctionType
+MULT = mybir.AluOpType.mult
+
+P = 128
+PACK = 4
+PASSES = K // (P * PACK)
+CHUNK = 512
+CHUNKS = T // CHUNK
+GROUPS = F // 512
+BLOCKS = K // 32
+HALF = 256
+ACC_BANKS = 3
+TURN_BANKS = 3
+OUT_BANKS = 2
+
+
+def tile_cauchy_influence_steps_b13_kernel(tc, R_bytes, R_scale, X, inv_c, step, out_0, out_1, out_2):
+    nc = tc.nc
+    with ExitStack() as ctx:
+        sb = ctx.enter_context(tc.tile_pool(name="sb", bufs=1))
+        ps = ctx.enter_context(tc.psum_pool(name="ps", bufs=1))
+        ctx.enter_context(tc.manual_schedule())
+
+        park = out_0[T - 96 : T, :].rearrange("r n -> (r n)")
+        words_out = out_1.rearrange("g p m t -> g p (m t)").bitcast(I32)
+        scales_out = out_2.bitcast(I32)
+
+        r_raw, r_wide, x_raw, x_grouped, x_codes, x_scales = {}, {}, {}, {}, {}, {}
+        spread, turned, r_scaled, r_codes, r_scales = {}, {}, {}, {}, {}
+        acc, weight, y, y_turned, y_grouped = {}, {}, {}, {}, {}
+
+        warm = sb.tile([P, 1], F32, name="warm")
+        nc.gpsimd.memset(warm[:], 1.0)
+        warm_out = sb.tile([P, 1], F32, name="warm_out")
+        nc.scalar.activation(out=warm_out[:], in_=warm[:], func=ACT.Abs_reciprocal_sqrt, bias=1.0, scale=1.0)
+        ident = sb.tile([P, P], F32, name="ident")
+        make_identity(nc, ident[:])
+        y_scales = sb.tile([P, GROUPS, T], U8, name="y_scales", align_bytes=64)
+
+        def load_bytes(i):
+            r_raw[i] = sb.tile([P, K], U8, name="r_raw", bufs=12)
+            nc.sync.dma_start(out=r_raw[i][:], in_=R_bytes[P * i : P * (i + 1), :])
+
+        def load_x(G, g):
+            x_raw[G, g] = sb.tile([P, PACK, 512], BF16, name="x_raw", bufs=8)
+            rows = X[512 * g : 512 * (g + 1), 512 * G : 512 * (G + 1)]
+            nc.sync.dma_start(out=x_raw[G, g][:], in_=rows.rearrange("(p j) f -> p j f", j=PACK))
+
+        def load_scales(lo, hi, tag):
+            pairs = (hi - lo) // (2 * P)
+            raw = sb.tile([P, pairs, 2, BLOCKS], F32, name=tag)
+            for h in range(2):
+                rows = R_scale[lo + h * pairs * P : lo + (h + 1) * pairs * P, :]
+                nc.sync.dma_start(out=raw[:, :, h, :], in_=rows.rearrange("(j p) b -> p j b", p=P))
+            return raw
+
+        def park_scales(raw, lo, hi, tag):
+            pairs = (hi - lo) // (2 * P)
+            bank = ps.tile([P, PACK, P], F32, name="out_bank", bufs=OUT_BANKS)
+            for j in range(pairs):
+                nc.tensor.transpose(bank[:, j, :], raw[:, j, :, :].rearrange("p h b -> p (h b)"), ident[:])
+            rows = sb.tile([P, pairs, P], F32, name=tag)
+            nc.scalar.copy(out=rows[:], in_=bank[:, 0:pairs, :])
+            nc.scalar.dma_start(out=parked(lo, hi), in_=rows[:].rearrange("q j p -> q (j p)"))
+
+        def parked(lo, hi):
+            return park[BLOCKS * lo : BLOCKS * hi].rearrange("(q m) -> q m", q=P)
+
+        def load_spread(lo, hi, h, tag):
+            width = (hi - lo) // 2
+            for g in range(PASSES):
+                t = sb.tile([P, width], F32, name=tag, bufs=2 * PASSES)
+                q0 = BLOCKS * h + 16 * g
+                nc.sync.dma_start(out=t[:], in_=parked(lo, hi)[q0 : q0 + 16, :].unsqueeze(1).to_broadcast([16, 8, width]))
+                for m in range(0, width, HALF):
+                    spread[(lo + h * width + m) // HALF, g] = t[:, m : m + HALF]
+
+        def widen(i, part):
+            if part == 0:
+                r_wide[i] = sb.tile([P, K], BF16, name="r_wide", bufs=8)
+            cols = slice(part * K // 2, (part + 1) * K // 2)
+            nc.scalar.copy(out=r_wide[i][:, cols], in_=r_raw[i][:, cols].bitcast(FP8))
+
+        def group_x(G, g):
+            x_grouped[G, g] = sb.tile([P, PACK * 512], BF16, name="x_grouped", bufs=3, align_bytes=64)
+            nc.vector.tensor_copy(
+                out=x_grouped[G, g][:].rearrange("p (t a e j) -> p a j e t", t=4, e=2, j=4),
+                in_=x_raw[G, g][:].rearrange("p j (a e t) -> p a j e t", e=2, t=4),
+            )
+
+        def quantize_x(G, g):
+            x_codes[G, g] = sb.tile([P, 512], U32, name="x_codes", bufs=8, align_bytes=64)
+            x_scales[G, g] = sb.tile([P, 512], U8, name="x_scales", bufs=8, align_bytes=64)
+            nc.vector.quantize_mx(out=x_codes[G, g][:].bitcast(E4X4), scales=x_scales[G, g][:], in_=x_grouped[G, g][:])
+
+        def turn_r(k):
+            half, g = divmod(k, PASSES)
+            turned[k] = ps.tile([P, 2, HALF], F32, name="turn_bank", bufs=TURN_BANKS)
+            for j in range(2):
+                words = r_wide[2 * half + j][:].bitcast(F32)
+                for u in range(2):
+                    nc.tensor.transpose(
+                        turned[k][:, u, P * j : P * (j + 1)], words[:, 256 * g + u : 256 * (g + 1) : 2], ident[:]
+                    )
+
+        def scale_r(k):
+            half, g = divmod(k, PASSES)
+            r_scaled[k] = sb.tile([P, HALF * PACK], BF16, name="r_scaled", bufs=3, align_bytes=64)
+            nc.vector.tensor_tensor(
+                out=r_scaled[k][:].rearrange("p (m u e) -> p m u e", u=2, e=2),
+                in0=turned[k][:].rearrange("p u m -> p (u m)").bitcast(BF16).rearrange("p (u m e) -> p m u e", u=2, e=2),
+                in1=spread[half, g].unsqueeze(2).unsqueeze(3).to_broadcast([P, HALF, 2, 2]),
+                op=MULT,
+            )
+            if k + TURN_BANKS < 2 * CHUNKS * PASSES:
+                pending_turns.append(k + TURN_BANKS)
+            issue_turns()
+
+        def quantize_r(k):
+            half, g = divmod(k, PASSES)
+            c, h = divmod(half, 2)
+            if h == 0:
+                r_codes[c, g] = sb.tile([P, CHUNK], U32, name="r_codes", bufs=8, align_bytes=64)
+                r_scales[c, g] = sb.tile([P, CHUNK], U8, name="r_scales", bufs=8, align_bytes=64)
+            cols = slice(HALF * h, HALF * (h + 1))
+            nc.vector.quantize_mx(
+                out=r_codes[c, g][:, cols].bitcast(E5X4), scales=r_scales[c, g][:, cols], in_=r_scaled[k][:]
+            )
+            done.add(("r", k))
+            issue_products()
+
+        pending_turns = []
+        done = set()
+        issued = []
+
+        def issue_turns():
+            for k in list(pending_turns):
+                if 2 * (k // PASSES) + 1 in r_wide and ("w", 2 * (k // PASSES) + 1) in done:
+                    turn_r(k)
+                    pending_turns.remove(k)
+
+        def issue_products():
+            for n in range(len(issued), 4 * GROUPS * CHUNKS):
+                unit, t = divmod(n, 4)
+                c, G = divmod(unit, GROUPS)
+                ready = ("r", 8 * c + 7) in done and (G, PASSES - 1) in x_codes
+                free = n < ACC_BANKS or ("y", n - ACC_BANKS) in done
+                if ready and free and len(issued) == n:
+                    acc[n] = ps.tile([P, CHUNK], F32, name="acc_bank", bufs=ACC_BANKS)
+                    cols = slice(P * t, P * (t + 1))
+                    for g in range(PASSES):
+                        nc.tensor.matmul_mx(
+                            out=acc[n][:],
+                            lhsT=x_codes[G, g][:, cols].bitcast(E4X4),
+                            lhsT_scale=x_scales[G, g][:, cols],
+                            rhs=r_codes[c, g][:].bitcast(E5X4),
+                            rhs_scale=r_scales[c, g][:],
+                            start=(g == 0),
+                            stop=(g == PASSES - 1),
+                        )
+                    issued.append(n)
+
+        def weigh(n, fill):
+            unit, t = divmod(n, 4)
+            col = 4 * (unit % GROUPS) + t
+            q = sb.tile([P, CHUNK], F32, name="q", bufs=2)
+            r = sb.tile([P, CHUNK], F32, name="r", bufs=2)
+            weight[n] = sb.tile([P, CHUNK], F32, name="weight", bufs=3)
+            parts = [slice(0, CHUNK)] if fill else [slice(0, HALF), slice(HALF, CHUNK)]
+            for s in parts:
+                nc.scalar.activation(out=q[:, s], in_=acc[n][:, s], func=ACT.Square, scale=a32[:, col : col + 1])
+            if fill:
+                fill(0)
+            for s in parts:
+                nc.scalar.activation(out=r[:, s], in_=q[:, s], func=ACT.Abs_reciprocal_sqrt, bias=1.0, scale=1.0)
+            if fill:
+                fill(1)
+            for s in parts:
+                nc.scalar.activation(out=weight[n][:, s], in_=r[:, s], func=ACT.Square)
+
+        def finish(n):
+            unit, t = divmod(n, 4)
+            col = 4 * (unit % GROUPS) + t
+            if t == 0:
+                y[unit] = sb.tile([P, PACK, CHUNK], F32, name="y", bufs=3)
+            nc.vector.scalar_tensor_tensor(
+                out=y[unit][:, t, :], in0=acc[n][:], scalar=c32[:, col : col + 1], in1=weight[n][:], op0=MULT, op1=MULT
+            )
+            done.add(("y", n))
+            issue_y_turns()
+            issue_products()
+
+        def turn_y(unit, i):
+            y_turned[unit, i] = ps.tile([P, PACK, P], F32, name="out_bank", bufs=OUT_BANKS)
+            for t in range(PACK):
+                nc.tensor.transpose(y_turned[unit, i][:, t, :], y[unit][:, t, P * i : P * (i + 1)], ident[:])
+
+        def issue_y_turns():
+            for n in range(len(y_turned), 4 * GROUPS * CHUNKS):
+                unit, i = divmod(n, 4)
+                free = n < OUT_BANKS or ("o", n - OUT_BANKS) in done
+                if free and ("y", 4 * unit + 3) in done and len(y_turned) == n:
+                    turn_y(unit, i)
+
+        rows_out = {}
+
+        def empty_y(unit, i, part, engine):
+            c, G = divmod(unit, GROUPS)
+            if part in (0, None):
+                rows_out[unit, i] = sb.tile([P, P, PACK], F32, name="rows_out", bufs=4)
+            s = slice(0, P) if part is None else slice(64 * part, 64 * (part + 1))
+            src = y_turned[unit, i][:].rearrange("p t m -> p m t")[:, s, :]
+            if engine == "scalar":
+                nc.scalar.copy(out=rows_out[unit, i][:, s, :], in_=src)
+            else:
+                nc.vector.tensor_copy(out=rows_out[unit, i][:, s, :], in_=src)
+            if part in (1, None):
+                m0 = CHUNK * c + P * i
+                nc.sync.dma_start(
+                    out=out_0[m0 : m0 + P, 512 * G : 512 * (G + 1)], in_=rows_out[unit, i][:].rearrange("p m t -> p (m t)")
+                )
+                done.add(("o", 4 * unit + i))
+                issue_y_turns()
+
+        def group_y(unit):
+            y_grouped[unit] = sb.tile([P, CHUNK * PACK], BF16, name="y_grouped", bufs=1, align_bytes=64)
+            nc.vector.tensor_copy(
+                out=y_grouped[unit][:].rearrange("p (a i t) -> p a t i", i=4, t=4),
+                in_=y[unit][:].rearrange("p t (a i) -> p a t i", i=4),
+            )
+
+        def quantize_y(unit):
+            c, G = divmod(unit, GROUPS)
+            cols = slice(CHUNK * c, CHUNK * (c + 1))
+            y_codes = sb.tile([P, CHUNK], U32, name="y_codes", bufs=2, align_bytes=64)
+            nc.vector.quantize_mx(out=y_codes[:].bitcast(E4X4), scales=y_scales[:, G, cols], in_=y_grouped[unit][:])
+            nc.sync.dma_start(out=words_out[G][:, cols], in_=y_codes[:].bitcast(I32))
+
+        def store_scales(c0, c1):
+            for Q in range(4):
+                nc.sync.dma_start(
+                    out=scales_out[:, 4 * Q : 4 * Q + 4, P * c0 : P * c1].rearrange("g r m -> r g m"),
+                    in_=y_scales[32 * Q : 32 * Q + 4, :, CHUNK * c0 : CHUNK * c1].bitcast(I32),
+                )
+
+        def widen_whole(i):
+            widen(i, 0)
+            widen(i, 1)
+            done.add(("w", i))
+            issue_turns()
+
+        def widen_fill(i):
+            def fill(part):
+                widen(i, part)
+                if part == 1:
+                    done.add(("w", i))
+            return fill
+
+        def empty_fill(unit, i):
+            def fill(part):
+                empty_y(unit, i, part, "scalar")
+            return fill
+
+        first_scales = load_scales(0, CHUNK, "scale_first")
+        for g in range(3):
+            load_x(0, g)
+            load_bytes(g)
+        park_scales(first_scales, 0, CHUNK, "scale_rows_first")
+        load_x(0, 3)
+        load_bytes(3)
+        load_spread(0, CHUNK, 0, "spread_first")
+        load_bytes(4)
+        load_spread(0, CHUNK, 1, "spread_first")
+        rest_scales = load_scales(CHUNK, T, "scale_rest")
+        load_bytes(5)
+        inv_c_sb = sb.tile([P, GROUPS, PACK], BF16, name="inv_c_sb")
+        step_sb = sb.tile([P, GROUPS, PACK], BF16, name="step_sb")
+        nc.sync.dma_start(out=inv_c_sb[:], in_=inv_c.rearrange("o (g p t) -> p (o g) t", p=P, t=PACK))
+        nc.sync.dma_start(out=step_sb[:], in_=step.rearrange("o (g p t) -> p (o g) t", p=P, t=PACK))
+        load_bytes(6)
+        load_bytes(7)
+
+        pending_turns.extend(range(TURN_BANKS))
+        for i in range(6):
+            widen_whole(i)
+        park_scales(rest_scales, CHUNK, T, "scale_rows_rest")
+        for g in range(PASSES):
+            load_x(1, g)
+            load_bytes(8 + g)
+        for h in range(2):
+            load_spread(CHUNK, T, h, "spread_rest")
+        for i in range(6, 8):
+            widen_whole(i)
+
+        group_x(0, 0)
+        for g in range(1, PASSES):
+            group_x(0, g)
+            quantize_x(0, g - 1)
+        scale_r(0)
+        quantize_x(0, PASSES - 1)
+        for k in range(1, 8):
+            scale_r(k)
+            if k == 1:
+                widen_whole(8)
+            quantize_r(k - 1)
+        a32 = sb.tile([P, GROUPS * PACK], F32, name="a32")
+        c32 = sb.tile([P, GROUPS * PACK], F32, name="c32")
+        nc.vector.tensor_copy(out=a32[:], in_=inv_c_sb[:].rearrange("p g t -> p (g t)"))
+        nc.vector.tensor_tensor(
+            out=c32[:], in0=inv_c_sb[:].rearrange("p g t -> p (g t)"), in1=step_sb[:].rearrange("p g t -> p (g t)"), op=MULT
+        )
+        quantize_r(7)
+
+        def qx(G, g):
+            quantize_x(G, g)
+            issue_products()
+
+        supply = {
+            0: [(group_x, 1, 0), (group_x, 1, 1), (qx, 1, 0), (group_x, 1, 2), (qx, 1, 1)],
+            1: [(group_x, 1, 3), (qx, 1, 2), (scale_r, 8), (qx, 1, 3)],
+            2: [(scale_r, 9), (quantize_r, 8), (scale_r, 10), (quantize_r, 9)],
+            3: [(scale_r, 11), (quantize_r, 10), (scale_r, 12), (quantize_r, 11)],
+            4: [(scale_r, 13), (quantize_r, 12)],
+            5: [(scale_r, 14), (quantize_r, 13), (scale_r, 15), (quantize_r, 14)],
+            6: [(quantize_r, 15)],
+            7: [(scale_r, 16)],
+            8: [(scale_r, 17), (quantize_r, 16), (scale_r, 18), (quantize_r, 17)],
+            9: [(scale_r, 19), (quantize_r, 18)],
+            10: [(group_y, 0), (scale_r, 20), (quantize_r, 19), (quantize_y, 0)],
+            11: [(scale_r, 21), (quantize_r, 20)],
+            12: [(scale_r, 22), (quantize_r, 21)],
+            13: [(scale_r, 23), (quantize_r, 22)],
+            14: [(quantize_r, 23), (group_y, 1)],
+            15: [(quantize_y, 1)],
+            16: [(group_y, 2)],
+            17: [(quantize_y, 2), (empty_y, 3, 0, None, "vector")],
+            18: [(empty_y, 3, 1, None, "vector"), (group_y, 3)],
+            19: [(empty_y, 3, 2, None, "vector"), (quantize_y, 3), (store_scales, 0, 2)],
+            20: [(empty_y, 3, 3, None, "vector")],
+            21: [(empty_y, 4, 0, None, "vector"), (group_y, 4)],
+            22: [(empty_y, 4, 1, None, "vector"), (quantize_y, 4), (empty_y, 4, 2, None, "vector")],
+            23: [(empty_y, 4, 3, None, "vector")],
+        }
+        for n in range(4 * GROUPS * CHUNKS):
+            for item in supply[n]:
+                item[0](*item[1:])
+            if n < 3:
+                fill = widen_fill(9 + n)
+            elif 5 <= n <= 16:
+                fill = empty_fill(*divmod(n - 5, 4))
+            else:
+                fill = None
+            weigh(n, fill)
+            issue_turns()
+            finish(n)
+
+        last = GROUPS * CHUNKS - 1
+        group_y(last)
+        for i in range(4):
+            empty_y(last, i, None, "scalar")
+        quantize_y(last)
+        store_scales(2, 3)

@@ -28,6 +28,8 @@ HALF = 256
 ACC_BANKS = 3
 TURN_BANKS = 3
 OUT_BANKS = 2
+STEPS = 4 * GROUPS * CHUNKS
+PLAN = [[[["b",8],["b",9],["b",10],["b",11]],[["b",12],["b",13],["b",14]],[["qx",1,1],["qx",1,2],["qx",1,3]],[["qr",8],["wv",10]],[["gy",0],["b",15],["b",16]],[["b",17]],[["qr",12]],[["qy",0],["wv",11]],[["gy",1],["b",18],["b",19]],[["b",20]],[["qr",16]],[["qy",1]],[["gy",2],["b",21],["b",22]],[["b",23]],[["qr",20],["hv",9]],[["qy",2],["hv",10]],[["gy",3],["hv",11]],[["hv",12]],[["hv",13],["qy",3],["ss",0,2]],[["hv",14]],[["gy",4],["hv",15]],[["hv",16],["hv",17]],[["qy",4],["ph",0],["hs",18],["qh",0]],[["hv",20]],[["hs",19],["ph",1],["hs",21],["qh",1],["hs",22],["hv",23],["ss",2,3]]],[None,["w",8],None,["w",9],None,["h",0],["h",1],["h",2],["h",3],["h",4],["h",5],["h",6],["h",7],["h",8],None,None,None,None,None,None,None,None,None,None]]
 
 
 def tile_cauchy_influence_steps_b13_kernel(tc, R_bytes, R_scale, X, inv_c, step, out_0, out_1, out_2):
@@ -54,11 +56,11 @@ def tile_cauchy_influence_steps_b13_kernel(tc, R_bytes, R_scale, X, inv_c, step,
         y_scales = sb.tile([P, GROUPS, T], U8, name="y_scales", align_bytes=64)
 
         def load_bytes(i):
-            r_raw[i] = sb.tile([P, K], U8, name="r_raw", bufs=12)
+            r_raw[i] = sb.tile([P, K], U8, name="r_raw", bufs=10)
             nc.sync.dma_start(out=r_raw[i][:], in_=R_bytes[P * i : P * (i + 1), :])
 
         def load_x(G, g):
-            x_raw[G, g] = sb.tile([P, PACK, 512], BF16, name="x_raw", bufs=8)
+            x_raw[G, g] = sb.tile([P, PACK, 512], BF16, name="x_raw", bufs=5)
             rows = X[512 * g : 512 * (g + 1), 512 * G : 512 * (G + 1)]
             nc.sync.dma_start(out=x_raw[G, g][:], in_=rows.rearrange("(p j) f -> p j f", j=PACK))
 
@@ -97,11 +99,19 @@ def tile_cauchy_influence_steps_b13_kernel(tc, R_bytes, R_scale, X, inv_c, step,
             cols = slice(part * K // 2, (part + 1) * K // 2)
             nc.scalar.copy(out=r_wide[i][:, cols], in_=r_raw[i][:, cols].bitcast(FP8))
 
-        def group_x(G, g):
-            x_grouped[G, g] = sb.tile([P, PACK * 512], BF16, name="x_grouped", bufs=3, align_bytes=64)
+        def group_x(G, g, tag):
+            x_grouped[G, g] = sb.tile([P, PACK * 512], BF16, name=tag, bufs=1, align_bytes=64)
             nc.vector.tensor_copy(
                 out=x_grouped[G, g][:].rearrange("p (t a e j) -> p a j e t", t=4, e=2, j=4),
                 in_=x_raw[G, g][:].rearrange("p j (a e t) -> p a j e t", e=2, t=4),
+            )
+
+        def group_x_pool(G, g, tag):
+            x_grouped[G, g] = sb.tile([P, PACK * 512], BF16, name=tag, bufs=1, align_bytes=64)
+            nc.gpsimd.tensor_scalar(
+                out=x_grouped[G, g][:].rearrange("p (t m j) -> p t m j", t=4, j=4),
+                in0=x_raw[G, g][:].rearrange("p j (m t) -> p t m j", t=4),
+                scalar1=1.0, scalar2=1.0, op0=MULT, op1=MULT,
             )
 
         def quantize_x(G, g):
@@ -121,7 +131,7 @@ def tile_cauchy_influence_steps_b13_kernel(tc, R_bytes, R_scale, X, inv_c, step,
 
         def scale_r(k):
             half, g = divmod(k, PASSES)
-            r_scaled[k] = sb.tile([P, HALF * PACK], BF16, name="r_scaled", bufs=3, align_bytes=64)
+            r_scaled[k] = sb.tile([P, HALF * PACK], BF16, name="r_scaled", bufs=8, align_bytes=64)
             nc.vector.tensor_tensor(
                 out=r_scaled[k][:].rearrange("p (m u e) -> p m u e", u=2, e=2),
                 in0=turned[k][:].rearrange("p u m -> p (u m)").bitcast(BF16).rearrange("p (u m e) -> p m u e", u=2, e=2),
@@ -160,9 +170,14 @@ def tile_cauchy_influence_steps_b13_kernel(tc, R_bytes, R_scale, X, inv_c, step,
                 unit, t = divmod(n, 4)
                 c, G = divmod(unit, GROUPS)
                 ready = ("r", 8 * c + 7) in done and (G, PASSES - 1) in x_codes
-                free = n < ACC_BANKS or ("y", n - ACC_BANKS) in done
+                late = n >= STEPS - 8
+                spare = late and n % 2 == 1
+                free = n < ACC_BANKS or ("y", max(n - 5, 5 + n // 2 if not spare else 0) if late else n - ACC_BANKS) in done
                 if ready and free and len(issued) == n:
-                    acc[n] = ps.tile([P, CHUNK], F32, name="acc_bank", bufs=ACC_BANKS)
+                    if spare:
+                        acc[n] = ps.tile([P, CHUNK], F32, name="turn_bank", bufs=TURN_BANKS)
+                    else:
+                        acc[n] = ps.tile([P, CHUNK], F32, name="acc_bank", bufs=ACC_BANKS)
                     cols = slice(P * t, P * (t + 1))
                     for g in range(PASSES):
                         nc.tensor.matmul_mx(
@@ -181,7 +196,7 @@ def tile_cauchy_influence_steps_b13_kernel(tc, R_bytes, R_scale, X, inv_c, step,
             col = 4 * (unit % GROUPS) + t
             q = sb.tile([P, CHUNK], F32, name="q", bufs=2)
             r = sb.tile([P, CHUNK], F32, name="r", bufs=2)
-            weight[n] = sb.tile([P, CHUNK], F32, name="weight", bufs=3)
+            weight[n] = sb.tile([P, CHUNK], F32, name="weight", bufs=4)
             parts = [slice(0, CHUNK)] if fill else [slice(0, HALF), slice(HALF, CHUNK)]
             for s in parts:
                 nc.scalar.activation(out=q[:, s], in_=acc[n][:, s], func=ACT.Square, scale=a32[:, col : col + 1])
@@ -203,19 +218,30 @@ def tile_cauchy_influence_steps_b13_kernel(tc, R_bytes, R_scale, X, inv_c, step,
                 out=y[unit][:, t, :], in0=acc[n][:], scalar=c32[:, col : col + 1], in1=weight[n][:], op0=MULT, op1=MULT
             )
             done.add(("y", n))
+            done.add(("y", n, 0))
+            done.add(("y", n, 1))
             issue_y_turns()
             issue_products()
 
         def turn_y(unit, i):
-            y_turned[unit, i] = ps.tile([P, PACK, P], F32, name="out_bank", bufs=OUT_BANKS)
+            if unit >= 4 and i == 2:
+                y_turned[unit, i] = ps.tile([P, PACK, P], F32, name="acc_bank", bufs=ACC_BANKS)
+            elif unit >= 4 and i == 3:
+                y_turned[unit, i] = ps.tile([P, PACK, P], F32, name="turn_bank", bufs=TURN_BANKS)
+            else:
+                y_turned[unit, i] = ps.tile([P, PACK, P], F32, name="out_bank", bufs=OUT_BANKS)
             for t in range(PACK):
-                nc.tensor.transpose(y_turned[unit, i][:, t, :], y[unit][:, t, P * i : P * (i + 1)], ident[:])
+                if unit == GROUPS * CHUNKS - 1:
+                    src = y[unit, i // 2][:, t, P * (i % 2) : P * (i % 2 + 1)]
+                else:
+                    src = y[unit][:, t, P * i : P * (i + 1)]
+                nc.tensor.transpose(y_turned[unit, i][:, t, :], src, ident[:])
 
         def issue_y_turns():
             for n in range(len(y_turned), 4 * GROUPS * CHUNKS):
                 unit, i = divmod(n, 4)
-                free = n < OUT_BANKS or ("o", n - OUT_BANKS) in done
-                if free and ("y", 4 * unit + 3) in done and len(y_turned) == n:
+                free = n < OUT_BANKS or n in (18, 19) or ("o", n - (4 if n >= 20 else OUT_BANKS)) in done
+                if free and ("y", 4 * unit + 3, i // 2) in done and len(y_turned) == n:
                     turn_y(unit, i)
 
         rows_out = {}
@@ -223,7 +249,7 @@ def tile_cauchy_influence_steps_b13_kernel(tc, R_bytes, R_scale, X, inv_c, step,
         def empty_y(unit, i, part, engine):
             c, G = divmod(unit, GROUPS)
             if part in (0, None):
-                rows_out[unit, i] = sb.tile([P, P, PACK], F32, name="rows_out", bufs=4)
+                rows_out[unit, i] = sb.tile([P, P, PACK], F32, name="rows_out", bufs=6)
             s = slice(0, P) if part is None else slice(64 * part, 64 * (part + 1))
             src = y_turned[unit, i][:].rearrange("p t m -> p m t")[:, s, :]
             if engine == "scalar":
@@ -245,6 +271,20 @@ def tile_cauchy_influence_steps_b13_kernel(tc, R_bytes, R_scale, X, inv_c, step,
                 in_=y[unit][:].rearrange("p t (a i) -> p a t i", i=4),
             )
 
+        def group_y_pool(unit):
+            y_grouped[unit] = sb.tile([P, CHUNK * PACK], BF16, name="y_grouped", bufs=1, align_bytes=64)
+            nc.gpsimd.tensor_scalar(
+                out=y_grouped[unit][:].rearrange("p (a i t) -> p a t i", i=4, t=4),
+                in0=y[unit][:].rearrange("p t (a i) -> p a t i", i=4),
+                scalar1=1.0, scalar2=1.0, op0=MULT, op1=MULT,
+            )
+
+        def widen_vector(i):
+            r_wide[i] = sb.tile([P, K], BF16, name="r_wide", bufs=8)
+            nc.vector.tensor_copy(out=r_wide[i][:], in_=r_raw[i][:].bitcast(FP8))
+            done.add(("w", i))
+            issue_turns()
+
         def quantize_y(unit):
             c, G = divmod(unit, GROUPS)
             cols = slice(CHUNK * c, CHUNK * (c + 1))
@@ -252,9 +292,9 @@ def tile_cauchy_influence_steps_b13_kernel(tc, R_bytes, R_scale, X, inv_c, step,
             nc.vector.quantize_mx(out=y_codes[:].bitcast(E4X4), scales=y_scales[:, G, cols], in_=y_grouped[unit][:])
             nc.sync.dma_start(out=words_out[G][:, cols], in_=y_codes[:].bitcast(I32))
 
-        def store_scales(c0, c1):
+        def store_scales(c0, c1, queue):
             for Q in range(4):
-                nc.sync.dma_start(
+                queue.dma_start(
                     out=scales_out[:, 4 * Q : 4 * Q + 4, P * c0 : P * c1].rearrange("g r m -> r g m"),
                     in_=y_scales[32 * Q : 32 * Q + 4, :, CHUNK * c0 : CHUNK * c1].bitcast(I32),
                 )
@@ -277,102 +317,142 @@ def tile_cauchy_influence_steps_b13_kernel(tc, R_bytes, R_scale, X, inv_c, step,
                 empty_y(unit, i, part, "scalar")
             return fill
 
+        load_x(0, 0)
         first_scales = load_scales(0, CHUNK, "scale_first")
-        for g in range(3):
-            load_x(0, g)
-            load_bytes(g)
+        load_bytes(0)
+        load_x(0, 1)
+        load_bytes(1)
+        load_x(0, 2)
+        load_bytes(2)
         park_scales(first_scales, 0, CHUNK, "scale_rows_first")
         load_x(0, 3)
         load_bytes(3)
         load_spread(0, CHUNK, 0, "spread_first")
+        rest_scales = load_scales(CHUNK, T, "scale_rest")
+        load_x(1, 0)
         load_bytes(4)
         load_spread(0, CHUNK, 1, "spread_first")
-        rest_scales = load_scales(CHUNK, T, "scale_rest")
-        load_bytes(5)
         inv_c_sb = sb.tile([P, GROUPS, PACK], BF16, name="inv_c_sb")
         step_sb = sb.tile([P, GROUPS, PACK], BF16, name="step_sb")
+
+        group_x(0, 0, "xg_a")
+        group_x(0, 1, "xg_b")
+        quantize_x(0, 0)
+        group_x(0, 2, "xg_c")
+        quantize_x(0, 1)
+        quantize_x(0, 2)
+        load_bytes(5)
+        load_x(1, 1)
+        load_bytes(6)
         nc.sync.dma_start(out=inv_c_sb[:], in_=inv_c.rearrange("o (g p t) -> p (o g) t", p=P, t=PACK))
         nc.sync.dma_start(out=step_sb[:], in_=step.rearrange("o (g p t) -> p (o g) t", p=P, t=PACK))
-        load_bytes(6)
         load_bytes(7)
+        group_x_pool(0, 3, "xg_c")
+        group_x_pool(1, 0, "xg_a")
 
         pending_turns.extend(range(TURN_BANKS))
-        for i in range(6):
+        for i in range(5):
             widen_whole(i)
+        scale_r(0)
+        scale_r(1)
         park_scales(rest_scales, CHUNK, T, "scale_rows_rest")
-        for g in range(PASSES):
-            load_x(1, g)
-            load_bytes(8 + g)
-        for h in range(2):
-            load_spread(CHUNK, T, h, "spread_rest")
-        for i in range(6, 8):
+        load_x(1, 2)
+        load_spread(CHUNK, T, 0, "spread_rest")
+        load_bytes(8)
+        load_x(1, 3)
+        load_bytes(9)
+        load_bytes(10)
+        load_bytes(11)
+        load_spread(CHUNK, T, 1, "spread_rest")
+        for i in range(5, 8):
             widen_whole(i)
 
-        group_x(0, 0)
-        for g in range(1, PASSES):
-            group_x(0, g)
-            quantize_x(0, g - 1)
-        scale_r(0)
-        quantize_x(0, PASSES - 1)
-        for k in range(1, 8):
+        for k in range(2, 8):
             scale_r(k)
-            if k == 1:
-                widen_whole(8)
-            quantize_r(k - 1)
         a32 = sb.tile([P, GROUPS * PACK], F32, name="a32")
         c32 = sb.tile([P, GROUPS * PACK], F32, name="c32")
         nc.vector.tensor_copy(out=a32[:], in_=inv_c_sb[:].rearrange("p g t -> p (g t)"))
         nc.vector.tensor_tensor(
             out=c32[:], in0=inv_c_sb[:].rearrange("p g t -> p (g t)"), in1=step_sb[:].rearrange("p g t -> p (g t)"), op=MULT
         )
-        quantize_r(7)
+        quantize_x(0, 3)
+        for g in range(PASSES):
+            quantize_r(g)
+            quantize_r(PASSES + g)
+        quantize_x(1, 0)
+        group_x_pool(1, 1, "xg_a")
+        group_x_pool(1, 2, "xg_b")
+        group_x_pool(1, 3, "xg_c")
 
         def qx(G, g):
             quantize_x(G, g)
             issue_products()
 
-        supply = {
-            0: [(group_x, 1, 0), (group_x, 1, 1), (qx, 1, 0), (group_x, 1, 2), (qx, 1, 1)],
-            1: [(group_x, 1, 3), (qx, 1, 2), (scale_r, 8), (qx, 1, 3)],
-            2: [(scale_r, 9), (quantize_r, 8), (scale_r, 10), (quantize_r, 9)],
-            3: [(scale_r, 11), (quantize_r, 10), (scale_r, 12), (quantize_r, 11)],
-            4: [(scale_r, 13), (quantize_r, 12)],
-            5: [(scale_r, 14), (quantize_r, 13), (scale_r, 15), (quantize_r, 14)],
-            6: [(quantize_r, 15)],
-            7: [(scale_r, 16)],
-            8: [(scale_r, 17), (quantize_r, 16), (scale_r, 18), (quantize_r, 17)],
-            9: [(scale_r, 19), (quantize_r, 18)],
-            10: [(group_y, 0), (scale_r, 20), (quantize_r, 19), (quantize_y, 0)],
-            11: [(scale_r, 21), (quantize_r, 20)],
-            12: [(scale_r, 22), (quantize_r, 21)],
-            13: [(scale_r, 23), (quantize_r, 22)],
-            14: [(quantize_r, 23), (group_y, 1)],
-            15: [(quantize_y, 1)],
-            16: [(group_y, 2)],
-            17: [(quantize_y, 2), (empty_y, 3, 0, None, "vector")],
-            18: [(empty_y, 3, 1, None, "vector"), (group_y, 3)],
-            19: [(empty_y, 3, 2, None, "vector"), (quantize_y, 3), (store_scales, 0, 2)],
-            20: [(empty_y, 3, 3, None, "vector")],
-            21: [(empty_y, 4, 0, None, "vector"), (group_y, 4)],
-            22: [(empty_y, 4, 1, None, "vector"), (quantize_y, 4), (empty_y, 4, 2, None, "vector")],
-            23: [(empty_y, 4, 3, None, "vector")],
-        }
-        for n in range(4 * GROUPS * CHUNKS):
-            for item in supply[n]:
-                item[0](*item[1:])
-            if n < 3:
-                fill = widen_fill(9 + n)
-            elif 5 <= n <= 16:
-                fill = empty_fill(*divmod(n - 5, 4))
-            else:
-                fill = None
-            weigh(n, fill)
-            issue_turns()
-            finish(n)
+        def qr(k0):
+            for k in range(k0, k0 + 4):
+                quantize_r(k)
+
+        def hv(n):
+            empty_y(n // 4, n % 4, None, "vector")
 
         last = GROUPS * CHUNKS - 1
-        group_y(last)
-        for i in range(4):
-            empty_y(last, i, None, "scalar")
-        quantize_y(last)
-        store_scales(2, 3)
+
+        def weigh_pair(h, t0):
+            s = slice(HALF * h, HALF * (h + 1))
+            q, r, w = {}, {}, {}
+            if t0 == 0:
+                y[last, h] = sb.tile([P, PACK, HALF], F32, name="y", bufs=3)
+            for t in (t0, t0 + 1):
+                q[t] = sb.tile([P, HALF], F32, name="q", bufs=2)
+                nc.scalar.activation(out=q[t][:], in_=acc[4 * last + t][:, s], func=ACT.Square, scale=a32[:, 4 + t : 5 + t])
+            for t in (t0, t0 + 1):
+                r[t] = sb.tile([P, HALF], F32, name="r", bufs=2)
+                nc.scalar.activation(out=r[t][:], in_=q[t][:], func=ACT.Abs_reciprocal_sqrt, bias=1.0, scale=1.0)
+            for t in (t0, t0 + 1):
+                w[t] = sb.tile([P, HALF], F32, name="weight", bufs=4)
+                nc.scalar.activation(out=w[t][:], in_=r[t][:], func=ACT.Square)
+                nc.vector.scalar_tensor_tensor(
+                    out=y[last, h][:, t, :], in0=acc[4 * last + t][:, s], scalar=c32[:, 4 + t : 5 + t], in1=w[t][:], op0=MULT, op1=MULT
+                )
+            done.add(("y", 4 * last + t0 + 1, h))
+            issue_y_turns()
+
+        halves = {}
+
+        def planes_half(h):
+            s = slice(HALF * h, HALF * (h + 1))
+            grouped = sb.tile([P, HALF * PACK], BF16, name="y_grouped", bufs=1, align_bytes=64)
+            nc.vector.tensor_copy(
+                out=grouped[:].rearrange("p (a i t) -> p a t i", i=4, t=4),
+                in_=y[last, h][:].rearrange("p t (a i) -> p a t i", i=4),
+            )
+            halves[h] = grouped
+
+        def quantize_half(h):
+            cols = slice(T - CHUNK + HALF * h, T - CHUNK + HALF * (h + 1))
+            y_codes = sb.tile([P, HALF], U32, name="y_codes", bufs=2, align_bytes=64)
+            nc.vector.quantize_mx(out=y_codes[:].bitcast(E4X4), scales=y_scales[:, 1, cols], in_=halves[h][:])
+            nc.sync.dma_start(out=words_out[1][:, cols], in_=y_codes[:].bitcast(I32))
+
+        def hs(n):
+            empty_y(n // 4, n % 4, None, "scalar")
+
+        def ss(c0, c1):
+            store_scales(c0, c1, nc.sync if c0 == 0 else nc.scalar)
+
+        names = {"b": scale_r, "qx": qx, "qr": qr, "wv": widen_vector, "gy": group_y_pool, "qy": quantize_y, "hv": hv, "hs": hs,
+                 "ss": ss, "ph": planes_half, "qh": quantize_half, "gv": group_y}
+        supply, fills = PLAN
+        for n in range(STEPS + 1):
+            for item in supply[n]:
+                names[item[0]](*item[1:])
+            if n < STEPS - 4:
+                fill = None
+                if fills[n]:
+                    kind, j = fills[n]
+                    fill = widen_fill(j) if kind == "w" else empty_fill(j // 4, j % 4)
+                weigh(n, fill)
+                issue_turns()
+                finish(n)
+            elif n < STEPS:
+                weigh_pair((n % 4) // 2, 2 * (n % 2))

@@ -19,17 +19,23 @@ MULT = mybir.AluOpType.mult
 
 P = 128
 PACK = 4
-PASSES = K // (P * PACK)
-CHUNK = 512
-CHUNKS = T // CHUNK
-GROUPS = F // 512
+SPAN = P * PACK
+PASSES = K // SPAN
 BLOCKS = K // 32
-HALF = 256
-ACC_BANKS = 3
-TURN_BANKS = 3
-OUT_BANKS = 2
-STEPS = 4 * GROUPS * CHUNKS
-PLAN = [[[["b",8],["b",9],["b",10],["b",11]],[["b",12],["b",13],["b",14]],[["qx",1,1],["qx",1,2],["qx",1,3]],[["qr",8],["wv",10]],[["gy",0],["b",15],["b",16]],[["b",17]],[["qr",12]],[["qy",0],["wv",11]],[["gy",1],["b",18],["b",19]],[["b",20]],[["qr",16]],[["qy",1]],[["gy",2],["b",21],["b",22]],[["b",23]],[["qr",20],["hv",9]],[["qy",2],["hv",10]],[["gy",3],["hv",11]],[["hv",12]],[["hv",13],["qy",3],["ss",0,2]],[["hv",14]],[["gy",4],["hv",15]],[["hv",16],["hv",17]],[["qy",4],["ph",0],["hs",18],["qh",0]],[["hv",20]],[["hs",19],["ph",1],["hs",21],["qh",1],["hs",22],["hv",23],["ss",2,3]]],[None,["w",8],None,["w",9],None,["h",0],["h",1],["h",2],["h",3],["h",4],["h",5],["h",6],["h",7],["h",8],None,None,None,None,None,None,None,None,None,None]]
+CHUNK = 512
+HALF = CHUNK // 2
+UNITS = (T // CHUNK) * (F // SPAN)
+STEPS = PACK * UNITS
+PIECES = (T // HALF) * PASSES
+LATE = STEPS - 2 * PACK
+LAST = UNITS - 1
+
+ACC_BANKS, TURN_BANKS, OUT_BANKS = 3, 3, 2
+
+PIECES_FIRST, PIECES_NEXT = (4, 3), (2, 1)
+EMPTY_LAG = 5
+HANDOVER = 14
+LATE_AHEAD = 5
 
 
 def tile_cauchy_influence_steps_b13_kernel(tc, R_bytes, R_scale, X, inv_c, step, out_0, out_1, out_2):
@@ -39,13 +45,14 @@ def tile_cauchy_influence_steps_b13_kernel(tc, R_bytes, R_scale, X, inv_c, step,
         ps = ctx.enter_context(tc.psum_pool(name="ps", bufs=1))
         ctx.enter_context(tc.manual_schedule())
 
-        park = out_0[T - 96 : T, :].rearrange("r n -> (r n)")
+        park = out_0[T - BLOCKS * T // F : T, :].rearrange("r n -> (r n)")
         words_out = out_1.rearrange("g p m t -> g p (m t)").bitcast(I32)
         scales_out = out_2.bitcast(I32)
 
-        r_raw, r_wide, x_raw, x_grouped, x_codes, x_scales = {}, {}, {}, {}, {}, {}
-        spread, turned, r_scaled, r_codes, r_scales = {}, {}, {}, {}, {}
-        acc, weight, y, y_turned, y_grouped = {}, {}, {}, {}, {}
+        r_raw, r_wide, spread, turned, r_scaled, r_codes, r_scales = {}, {}, {}, {}, {}, {}, {}
+        x_raw, x_grouped, x_codes, x_scales = {}, {}, {}, {}
+        acc, weight, y, y_turned, y_grouped, rows_out = {}, {}, {}, {}, {}, {}
+        widened, scaled, quantized, finished, emptied = set(), set(), set(), set(), set()
 
         warm = sb.tile([P, 1], F32, name="warm")
         nc.gpsimd.memset(warm[:], 1.0)
@@ -53,127 +60,141 @@ def tile_cauchy_influence_steps_b13_kernel(tc, R_bytes, R_scale, X, inv_c, step,
         nc.scalar.activation(out=warm_out[:], in_=warm[:], func=ACT.Abs_reciprocal_sqrt, bias=1.0, scale=1.0)
         ident = sb.tile([P, P], F32, name="ident")
         make_identity(nc, ident[:])
-        y_scales = sb.tile([P, GROUPS, T], U8, name="y_scales", align_bytes=64)
+        y_scales = sb.tile([P, F // SPAN, T], U8, name="y_scales", align_bytes=64)
 
         def load_bytes(i):
             r_raw[i] = sb.tile([P, K], U8, name="r_raw", bufs=10)
             nc.sync.dma_start(out=r_raw[i][:], in_=R_bytes[P * i : P * (i + 1), :])
 
         def load_x(G, g):
-            x_raw[G, g] = sb.tile([P, PACK, 512], BF16, name="x_raw", bufs=5)
-            rows = X[512 * g : 512 * (g + 1), 512 * G : 512 * (G + 1)]
+            x_raw[G, g] = sb.tile([P, PACK, SPAN], BF16, name="x_raw", bufs=5)
+            rows = X[SPAN * g : SPAN * (g + 1), SPAN * G : SPAN * (G + 1)]
             nc.sync.dma_start(out=x_raw[G, g][:], in_=rows.rearrange("(p j) f -> p j f", j=PACK))
 
-        def load_scales(lo, hi, tag):
+        def load_columns(vector, name):
+            columns = sb.tile([P, F // SPAN, PACK], BF16, name=name)
+            nc.sync.dma_start(out=columns[:], in_=vector.rearrange("o (g p t) -> p (o g) t", p=P, t=PACK))
+            return columns[:].rearrange("p g t -> p (g t)")
+
+        def load_scales(lo, hi, name):
             pairs = (hi - lo) // (2 * P)
-            raw = sb.tile([P, pairs, 2, BLOCKS], F32, name=tag)
+            raw = sb.tile([P, pairs, 2, BLOCKS], F32, name=name)
             for h in range(2):
                 rows = R_scale[lo + h * pairs * P : lo + (h + 1) * pairs * P, :]
                 nc.sync.dma_start(out=raw[:, :, h, :], in_=rows.rearrange("(j p) b -> p j b", p=P))
             return raw
 
-        def park_scales(raw, lo, hi, tag):
+        def parked(lo, hi):
+            return park[BLOCKS * lo : BLOCKS * hi].rearrange("(q m) -> q m", q=P)
+
+        def park_scales(raw, lo, hi, name):
             pairs = (hi - lo) // (2 * P)
             bank = ps.tile([P, PACK, P], F32, name="out_bank", bufs=OUT_BANKS)
             for j in range(pairs):
                 nc.tensor.transpose(bank[:, j, :], raw[:, j, :, :].rearrange("p h b -> p (h b)"), ident[:])
-            rows = sb.tile([P, pairs, P], F32, name=tag)
+            rows = sb.tile([P, pairs, P], F32, name=name)
             nc.scalar.copy(out=rows[:], in_=bank[:, 0:pairs, :])
             nc.scalar.dma_start(out=parked(lo, hi), in_=rows[:].rearrange("q j p -> q (j p)"))
 
-        def parked(lo, hi):
-            return park[BLOCKS * lo : BLOCKS * hi].rearrange("(q m) -> q m", q=P)
-
-        def load_spread(lo, hi, h, tag):
+        def load_spread(lo, hi, h, name):
             width = (hi - lo) // 2
             for g in range(PASSES):
-                t = sb.tile([P, width], F32, name=tag, bufs=2 * PASSES)
+                factors = sb.tile([P, width], F32, name=name, bufs=2 * PASSES)
                 q0 = BLOCKS * h + 16 * g
-                nc.sync.dma_start(out=t[:], in_=parked(lo, hi)[q0 : q0 + 16, :].unsqueeze(1).to_broadcast([16, 8, width]))
+                nc.sync.dma_start(out=factors[:], in_=parked(lo, hi)[q0 : q0 + 16, :].unsqueeze(1).to_broadcast([16, 8, width]))
                 for m in range(0, width, HALF):
-                    spread[(lo + h * width + m) // HALF, g] = t[:, m : m + HALF]
+                    spread[(lo + h * width + m) // HALF, g] = factors[:, m : m + HALF]
 
-        def widen(i, part):
-            if part == 0:
-                r_wide[i] = sb.tile([P, K], BF16, name="r_wide", bufs=8)
-            cols = slice(part * K // 2, (part + 1) * K // 2)
-            nc.scalar.copy(out=r_wide[i][:, cols], in_=r_raw[i][:, cols].bitcast(FP8))
-
-        def group_x(G, g, tag):
-            x_grouped[G, g] = sb.tile([P, PACK * 512], BF16, name=tag, bufs=1, align_bytes=64)
+        def group_x(G, g, name):
+            x_grouped[G, g] = sb.tile([P, PACK * SPAN], BF16, name=name, align_bytes=64)
             nc.vector.tensor_copy(
-                out=x_grouped[G, g][:].rearrange("p (t a e j) -> p a j e t", t=4, e=2, j=4),
-                in_=x_raw[G, g][:].rearrange("p j (a e t) -> p a j e t", e=2, t=4),
+                out=x_grouped[G, g][:].rearrange("p (t a e j) -> p a j e t", t=PACK, e=2, j=PACK),
+                in_=x_raw[G, g][:].rearrange("p j (a e t) -> p a j e t", e=2, t=PACK),
             )
 
-        def group_x_pool(G, g, tag):
-            x_grouped[G, g] = sb.tile([P, PACK * 512], BF16, name=tag, bufs=1, align_bytes=64)
+        def group_x_gpsimd(G, g, name):
+            x_grouped[G, g] = sb.tile([P, PACK * SPAN], BF16, name=name, align_bytes=64)
             nc.gpsimd.tensor_scalar(
-                out=x_grouped[G, g][:].rearrange("p (t m j) -> p t m j", t=4, j=4),
-                in0=x_raw[G, g][:].rearrange("p j (m t) -> p t m j", t=4),
+                out=x_grouped[G, g][:].rearrange("p (t m j) -> p t m j", t=PACK, j=PACK),
+                in0=x_raw[G, g][:].rearrange("p j (m t) -> p t m j", t=PACK),
                 scalar1=1.0, scalar2=1.0, op0=MULT, op1=MULT,
             )
 
         def quantize_x(G, g):
-            x_codes[G, g] = sb.tile([P, 512], U32, name="x_codes", bufs=8, align_bytes=64)
-            x_scales[G, g] = sb.tile([P, 512], U8, name="x_scales", bufs=8, align_bytes=64)
+            x_codes[G, g] = sb.tile([P, SPAN], U32, name="x_codes", bufs=2 * PASSES, align_bytes=64)
+            x_scales[G, g] = sb.tile([P, SPAN], U8, name="x_scales", bufs=2 * PASSES, align_bytes=64)
             nc.vector.quantize_mx(out=x_codes[G, g][:].bitcast(E4X4), scales=x_scales[G, g][:], in_=x_grouped[G, g][:])
-
-        def turn_r(k):
-            half, g = divmod(k, PASSES)
-            turned[k] = ps.tile([P, 2, HALF], F32, name="turn_bank", bufs=TURN_BANKS)
-            for j in range(2):
-                words = r_wide[2 * half + j][:].bitcast(F32)
-                for u in range(2):
-                    nc.tensor.transpose(
-                        turned[k][:, u, P * j : P * (j + 1)], words[:, 256 * g + u : 256 * (g + 1) : 2], ident[:]
-                    )
-
-        def scale_r(k):
-            half, g = divmod(k, PASSES)
-            r_scaled[k] = sb.tile([P, HALF * PACK], BF16, name="r_scaled", bufs=8, align_bytes=64)
-            nc.vector.tensor_tensor(
-                out=r_scaled[k][:].rearrange("p (m u e) -> p m u e", u=2, e=2),
-                in0=turned[k][:].rearrange("p u m -> p (u m)").bitcast(BF16).rearrange("p (u m e) -> p m u e", u=2, e=2),
-                in1=spread[half, g].unsqueeze(2).unsqueeze(3).to_broadcast([P, HALF, 2, 2]),
-                op=MULT,
-            )
-            if k + TURN_BANKS < 2 * CHUNKS * PASSES:
-                pending_turns.append(k + TURN_BANKS)
-            issue_turns()
-
-        def quantize_r(k):
-            half, g = divmod(k, PASSES)
-            c, h = divmod(half, 2)
-            if h == 0:
-                r_codes[c, g] = sb.tile([P, CHUNK], U32, name="r_codes", bufs=8, align_bytes=64)
-                r_scales[c, g] = sb.tile([P, CHUNK], U8, name="r_scales", bufs=8, align_bytes=64)
-            cols = slice(HALF * h, HALF * (h + 1))
-            nc.vector.quantize_mx(
-                out=r_codes[c, g][:, cols].bitcast(E5X4), scales=r_scales[c, g][:, cols], in_=r_scaled[k][:]
-            )
-            done.add(("r", k))
             issue_products()
 
-        pending_turns = []
-        done = set()
-        issued = []
+        def widen(i, parts, part):
+            if part == 0:
+                r_wide[i] = sb.tile([P, K], BF16, name="r_wide", bufs=8)
+            cols = slice(part * K // parts, (part + 1) * K // parts)
+            nc.scalar.copy(out=r_wide[i][:, cols], in_=r_raw[i][:, cols].bitcast(FP8))
+            if part == parts - 1:
+                widened.add(i)
+                issue_turns()
+
+        def widen_vector(i):
+            r_wide[i] = sb.tile([P, K], BF16, name="r_wide", bufs=8)
+            nc.vector.tensor_copy(out=r_wide[i][:], in_=r_raw[i][:].bitcast(FP8))
+            widened.add(i)
+            issue_turns()
 
         def issue_turns():
-            for k in list(pending_turns):
-                if 2 * (k // PASSES) + 1 in r_wide and ("w", 2 * (k // PASSES) + 1) in done:
-                    turn_r(k)
-                    pending_turns.remove(k)
+            for piece in range(len(turned), PIECES):
+                half, g = divmod(piece, PASSES)
+                free = piece < TURN_BANKS or piece - TURN_BANKS in scaled
+                if free and 2 * half + 1 in widened and len(turned) == piece:
+                    turned[piece] = ps.tile([P, 2, HALF], F32, name="turn_bank", bufs=TURN_BANKS)
+                    for j in range(2):
+                        words = r_wide[2 * half + j][:].bitcast(F32)
+                        for u in range(2):
+                            nc.tensor.transpose(
+                                turned[piece][:, u, P * j : P * (j + 1)],
+                                words[:, SPAN // 2 * g + u : SPAN // 2 * (g + 1) : 2],
+                                ident[:],
+                            )
+
+        def scale_r(count):
+            for piece in range(len(scaled), len(scaled) + count):
+                half, g = divmod(piece, PASSES)
+                r_scaled[piece] = sb.tile([P, HALF * PACK], BF16, name="r_scaled", bufs=2 * PASSES, align_bytes=64)
+                values = turned[piece][:].rearrange("p u m -> p (u m)").bitcast(BF16)
+                nc.vector.tensor_tensor(
+                    out=r_scaled[piece][:].rearrange("p (m u e) -> p m u e", u=2, e=2),
+                    in0=values.rearrange("p (u m e) -> p m u e", u=2, e=2),
+                    in1=spread[half, g].unsqueeze(2).unsqueeze(3).to_broadcast([P, HALF, 2, 2]),
+                    op=MULT,
+                )
+                scaled.add(piece)
+                issue_turns()
+
+        def quantize_r(half, g):
+            chunk, h = divmod(half, 2)
+            if h == 0:
+                r_codes[chunk, g] = sb.tile([P, CHUNK], U32, name="r_codes", bufs=2 * PASSES, align_bytes=64)
+                r_scales[chunk, g] = sb.tile([P, CHUNK], U8, name="r_scales", bufs=2 * PASSES, align_bytes=64)
+            cols = slice(HALF * h, HALF * (h + 1))
+            nc.vector.quantize_mx(
+                out=r_codes[chunk, g][:, cols].bitcast(E5X4), scales=r_scales[chunk, g][:, cols], in_=r_scaled[PASSES * half + g][:]
+            )
+            quantized.add((half, g))
+            issue_products()
 
         def issue_products():
-            for n in range(len(issued), 4 * GROUPS * CHUNKS):
-                unit, t = divmod(n, 4)
-                c, G = divmod(unit, GROUPS)
-                ready = ("r", 8 * c + 7) in done and (G, PASSES - 1) in x_codes
-                late = n >= STEPS - 8
-                spare = late and n % 2 == 1
-                free = n < ACC_BANKS or ("y", max(n - 5, 5 + n // 2 if not spare else 0) if late else n - ACC_BANKS) in done
-                if ready and free and len(issued) == n:
+            for n in range(len(acc), STEPS):
+                unit, t = divmod(n, PACK)
+                chunk, G = divmod(unit, 2)
+                spare = n >= LATE and n % 2 == 1
+                if n < LATE:
+                    after = n - ACC_BANKS
+                elif spare:
+                    after = n - LATE_AHEAD
+                else:
+                    after = max(n - LATE_AHEAD, LATE - ACC_BANKS + (n - LATE) // 2)
+                ready = (2 * chunk + 1, PASSES - 1) in quantized and (G, PASSES - 1) in x_codes
+                if ready and (after < 0 or after in finished) and len(acc) == n:
                     if spare:
                         acc[n] = ps.tile([P, CHUNK], F32, name="turn_bank", bufs=TURN_BANKS)
                     else:
@@ -184,275 +205,230 @@ def tile_cauchy_influence_steps_b13_kernel(tc, R_bytes, R_scale, X, inv_c, step,
                             out=acc[n][:],
                             lhsT=x_codes[G, g][:, cols].bitcast(E4X4),
                             lhsT_scale=x_scales[G, g][:, cols],
-                            rhs=r_codes[c, g][:].bitcast(E5X4),
-                            rhs_scale=r_scales[c, g][:],
+                            rhs=r_codes[chunk, g][:].bitcast(E5X4),
+                            rhs_scale=r_scales[chunk, g][:],
                             start=(g == 0),
                             stop=(g == PASSES - 1),
                         )
-                    issued.append(n)
 
-        def weigh(n, fill):
-            unit, t = divmod(n, 4)
-            col = 4 * (unit % GROUPS) + t
-            q = sb.tile([P, CHUNK], F32, name="q", bufs=2)
-            r = sb.tile([P, CHUNK], F32, name="r", bufs=2)
-            weight[n] = sb.tile([P, CHUNK], F32, name="weight", bufs=4)
-            parts = [slice(0, CHUNK)] if fill else [slice(0, HALF), slice(HALF, CHUNK)]
-            for s in parts:
-                nc.scalar.activation(out=q[:, s], in_=acc[n][:, s], func=ACT.Square, scale=a32[:, col : col + 1])
+        def weigh(jobs, width, fill):
+            square, root = {}, {}
+            for n, cols in jobs:
+                square[n, cols.start] = sb.tile([P, width], F32, name="square", bufs=2)
+                nc.scalar.activation(
+                    out=square[n, cols.start][:], in_=acc[n][:, cols], func=ACT.Square, scale=inv_c32[:, n % 8 : n % 8 + 1]
+                )
             if fill:
-                fill(0)
-            for s in parts:
-                nc.scalar.activation(out=r[:, s], in_=q[:, s], func=ACT.Abs_reciprocal_sqrt, bias=1.0, scale=1.0)
+                fill[0](*fill[1:], 0)
+            for n, cols in jobs:
+                root[n, cols.start] = sb.tile([P, width], F32, name="root", bufs=2)
+                nc.scalar.activation(
+                    out=root[n, cols.start][:], in_=square[n, cols.start][:], func=ACT.Abs_reciprocal_sqrt, bias=1.0, scale=1.0
+                )
             if fill:
-                fill(1)
-            for s in parts:
-                nc.scalar.activation(out=weight[n][:, s], in_=r[:, s], func=ACT.Square)
+                fill[0](*fill[1:], 1)
+            for n, cols in jobs:
+                if cols.start == 0 or n // PACK == LAST:
+                    weight[n] = sb.tile([P, CHUNK], F32, name="weight", bufs=4)
+                nc.scalar.activation(out=weight[n][:, cols], in_=root[n, cols.start][:], func=ACT.Square)
 
-        def finish(n):
-            unit, t = divmod(n, 4)
-            col = 4 * (unit % GROUPS) + t
-            if t == 0:
-                y[unit] = sb.tile([P, PACK, CHUNK], F32, name="y", bufs=3)
+        def finish(n, cols, result):
             nc.vector.scalar_tensor_tensor(
-                out=y[unit][:, t, :], in0=acc[n][:], scalar=c32[:, col : col + 1], in1=weight[n][:], op0=MULT, op1=MULT
+                out=result, in0=acc[n][:, cols], scalar=gain32[:, n % 8 : n % 8 + 1], in1=weight[n][:, cols], op0=MULT, op1=MULT
             )
-            done.add(("y", n))
-            done.add(("y", n, 0))
-            done.add(("y", n, 1))
-            issue_y_turns()
-            issue_products()
-
-        def turn_y(unit, i):
-            if unit >= 4 and i == 2:
-                y_turned[unit, i] = ps.tile([P, PACK, P], F32, name="acc_bank", bufs=ACC_BANKS)
-            elif unit >= 4 and i == 3:
-                y_turned[unit, i] = ps.tile([P, PACK, P], F32, name="turn_bank", bufs=TURN_BANKS)
-            else:
-                y_turned[unit, i] = ps.tile([P, PACK, P], F32, name="out_bank", bufs=OUT_BANKS)
-            for t in range(PACK):
-                if unit == GROUPS * CHUNKS - 1:
-                    src = y[unit, i // 2][:, t, P * (i % 2) : P * (i % 2 + 1)]
-                else:
-                    src = y[unit][:, t, P * i : P * (i + 1)]
-                nc.tensor.transpose(y_turned[unit, i][:, t, :], src, ident[:])
 
         def issue_y_turns():
-            for n in range(len(y_turned), 4 * GROUPS * CHUNKS):
-                unit, i = divmod(n, 4)
-                free = n < OUT_BANKS or n in (18, 19) or ("o", n - (4 if n >= 20 else OUT_BANKS)) in done
-                if free and ("y", 4 * unit + 3, i // 2) in done and len(y_turned) == n:
-                    turn_y(unit, i)
+            for j in range(len(y_turned), STEPS):
+                unit, i = divmod(j, PACK)
+                own_bank = j < LATE or i < OUT_BANKS
+                before = j - OUT_BANKS if j < LATE + OUT_BANKS else j - PACK
+                free = before < 0 or before in emptied or (not own_bank and unit < LAST)
+                if free and (unit, i // 2) in y and len(y_turned) == j:
+                    if own_bank:
+                        y_turned[j] = ps.tile([P, PACK, P], F32, name="out_bank", bufs=OUT_BANKS)
+                    elif i == 2:
+                        y_turned[j] = ps.tile([P, PACK, P], F32, name="acc_bank", bufs=ACC_BANKS)
+                    else:
+                        y_turned[j] = ps.tile([P, PACK, P], F32, name="turn_bank", bufs=TURN_BANKS)
+                    for t in range(PACK):
+                        nc.tensor.transpose(y_turned[j][:, t, :], y[unit, i // 2][:, t, P * (i % 2) : P * (i % 2 + 1)], ident[:])
 
-        rows_out = {}
-
-        def empty_y(unit, i, part, engine):
-            c, G = divmod(unit, GROUPS)
-            if part in (0, None):
-                rows_out[unit, i] = sb.tile([P, P, PACK], F32, name="rows_out", bufs=6)
-            s = slice(0, P) if part is None else slice(64 * part, 64 * (part + 1))
-            src = y_turned[unit, i][:].rearrange("p t m -> p m t")[:, s, :]
-            if engine == "scalar":
-                nc.scalar.copy(out=rows_out[unit, i][:, s, :], in_=src)
-            else:
-                nc.vector.tensor_copy(out=rows_out[unit, i][:, s, :], in_=src)
-            if part in (1, None):
-                m0 = CHUNK * c + P * i
+        def empty_y(j, copy, parts, part):
+            unit, i = divmod(j, PACK)
+            chunk, G = divmod(unit, 2)
+            if part == 0:
+                rows_out[j] = sb.tile([P, P, PACK], F32, name="rows_out", bufs=6)
+            cols = slice(part * P // parts, (part + 1) * P // parts)
+            copy(out=rows_out[j][:, cols, :], in_=y_turned[j][:].rearrange("p t m -> p m t")[:, cols, :])
+            if part == parts - 1:
+                m0 = CHUNK * chunk + P * i
                 nc.sync.dma_start(
-                    out=out_0[m0 : m0 + P, 512 * G : 512 * (G + 1)], in_=rows_out[unit, i][:].rearrange("p m t -> p (m t)")
+                    out=out_0[m0 : m0 + P, SPAN * G : SPAN * (G + 1)], in_=rows_out[j][:].rearrange("p m t -> p (m t)")
                 )
-                done.add(("o", 4 * unit + i))
+                emptied.add(j)
                 issue_y_turns()
 
-        def group_y(unit):
-            y_grouped[unit] = sb.tile([P, CHUNK * PACK], BF16, name="y_grouped", bufs=1, align_bytes=64)
-            nc.vector.tensor_copy(
-                out=y_grouped[unit][:].rearrange("p (a i t) -> p a t i", i=4, t=4),
-                in_=y[unit][:].rearrange("p t (a i) -> p a t i", i=4),
-            )
+        def empty_vector(j):
+            empty_y(j, nc.vector.tensor_copy, 1, 0)
 
-        def group_y_pool(unit):
-            y_grouped[unit] = sb.tile([P, CHUNK * PACK], BF16, name="y_grouped", bufs=1, align_bytes=64)
+        def empty_scalar(j):
+            empty_y(j, nc.scalar.copy, 1, 0)
+
+        def group_y_gpsimd(unit):
+            y_grouped[unit] = sb.tile([P, CHUNK * PACK], BF16, name="y_grouped", align_bytes=64)
             nc.gpsimd.tensor_scalar(
-                out=y_grouped[unit][:].rearrange("p (a i t) -> p a t i", i=4, t=4),
-                in0=y[unit][:].rearrange("p t (a i) -> p a t i", i=4),
+                out=y_grouped[unit][:].rearrange("p (m t) -> p m t", t=PACK),
+                in0=whole[unit][:].rearrange("p t m -> p m t"),
                 scalar1=1.0, scalar2=1.0, op0=MULT, op1=MULT,
             )
 
-        def widen_vector(i):
-            r_wide[i] = sb.tile([P, K], BF16, name="r_wide", bufs=8)
-            nc.vector.tensor_copy(out=r_wide[i][:], in_=r_raw[i][:].bitcast(FP8))
-            done.add(("w", i))
-            issue_turns()
+        def group_y_half(h):
+            y_grouped[LAST] = sb.tile([P, HALF * PACK], BF16, name="y_grouped", align_bytes=64)
+            nc.vector.tensor_copy(
+                out=y_grouped[LAST][:].rearrange("p (a i t) -> p a t i", i=4, t=PACK),
+                in_=y[LAST, h].rearrange("p t (a i) -> p a t i", i=4),
+            )
 
-        def quantize_y(unit):
-            c, G = divmod(unit, GROUPS)
-            cols = slice(CHUNK * c, CHUNK * (c + 1))
-            y_codes = sb.tile([P, CHUNK], U32, name="y_codes", bufs=2, align_bytes=64)
+        def quantize_y(unit, lo, hi):
+            chunk, G = divmod(unit, 2)
+            cols = slice(CHUNK * chunk + lo, CHUNK * chunk + hi)
+            y_codes = sb.tile([P, hi - lo], U32, name="y_codes", bufs=2, align_bytes=64)
             nc.vector.quantize_mx(out=y_codes[:].bitcast(E4X4), scales=y_scales[:, G, cols], in_=y_grouped[unit][:])
             nc.sync.dma_start(out=words_out[G][:, cols], in_=y_codes[:].bitcast(I32))
 
-        def store_scales(c0, c1, queue):
+        def store_scales(lo, hi, queue):
             for Q in range(4):
                 queue.dma_start(
-                    out=scales_out[:, 4 * Q : 4 * Q + 4, P * c0 : P * c1].rearrange("g r m -> r g m"),
-                    in_=y_scales[32 * Q : 32 * Q + 4, :, CHUNK * c0 : CHUNK * c1].bitcast(I32),
+                    out=scales_out[:, 4 * Q : 4 * Q + 4, lo // 4 : hi // 4].rearrange("g r m -> r g m"),
+                    in_=y_scales[32 * Q : 32 * Q + 4, :, lo:hi].bitcast(I32),
                 )
-
-        def widen_whole(i):
-            widen(i, 0)
-            widen(i, 1)
-            done.add(("w", i))
-            issue_turns()
-
-        def widen_fill(i):
-            def fill(part):
-                widen(i, part)
-                if part == 1:
-                    done.add(("w", i))
-            return fill
-
-        def empty_fill(unit, i):
-            def fill(part):
-                empty_y(unit, i, part, "scalar")
-            return fill
 
         load_x(0, 0)
         first_scales = load_scales(0, CHUNK, "scale_first")
         load_bytes(0)
-        load_x(0, 1)
-        load_bytes(1)
-        load_x(0, 2)
-        load_bytes(2)
+        for g in (1, 2):
+            load_x(0, g)
+            load_bytes(g)
         park_scales(first_scales, 0, CHUNK, "scale_rows_first")
         load_x(0, 3)
         load_bytes(3)
         load_spread(0, CHUNK, 0, "spread_first")
+        load_bytes(4)
         rest_scales = load_scales(CHUNK, T, "scale_rest")
         load_x(1, 0)
-        load_bytes(4)
         load_spread(0, CHUNK, 1, "spread_first")
-        inv_c_sb = sb.tile([P, GROUPS, PACK], BF16, name="inv_c_sb")
-        step_sb = sb.tile([P, GROUPS, PACK], BF16, name="step_sb")
 
-        group_x(0, 0, "xg_a")
-        group_x(0, 1, "xg_b")
+        group_x(0, 0, "x_grouped_a")
+        group_x(0, 1, "x_grouped_b")
         quantize_x(0, 0)
-        group_x(0, 2, "xg_c")
+        group_x(0, 2, "x_grouped_c")
         quantize_x(0, 1)
         quantize_x(0, 2)
+        group_x_gpsimd(0, 3, "x_grouped_c")
+        group_x_gpsimd(1, 0, "x_grouped_a")
+
         load_bytes(5)
         load_x(1, 1)
         load_bytes(6)
-        nc.sync.dma_start(out=inv_c_sb[:], in_=inv_c.rearrange("o (g p t) -> p (o g) t", p=P, t=PACK))
-        nc.sync.dma_start(out=step_sb[:], in_=step.rearrange("o (g p t) -> p (o g) t", p=P, t=PACK))
+        inv_c_sb = load_columns(inv_c, "inv_c_sb")
+        step_sb = load_columns(step, "step_sb")
         load_bytes(7)
-        group_x_pool(0, 3, "xg_c")
-        group_x_pool(1, 0, "xg_a")
-
-        pending_turns.extend(range(TURN_BANKS))
         for i in range(5):
-            widen_whole(i)
-        scale_r(0)
-        scale_r(1)
+            widen(i, 1, 0)
+        scale_r(2)
         park_scales(rest_scales, CHUNK, T, "scale_rows_rest")
         load_x(1, 2)
         load_spread(CHUNK, T, 0, "spread_rest")
         load_bytes(8)
         load_x(1, 3)
-        load_bytes(9)
-        load_bytes(10)
-        load_bytes(11)
+        for i in range(9, T // P):
+            load_bytes(i)
         load_spread(CHUNK, T, 1, "spread_rest")
         for i in range(5, 8):
-            widen_whole(i)
+            widen(i, 1, 0)
+        scale_r(2 * PASSES - 2)
 
-        for k in range(2, 8):
-            scale_r(k)
-        a32 = sb.tile([P, GROUPS * PACK], F32, name="a32")
-        c32 = sb.tile([P, GROUPS * PACK], F32, name="c32")
-        nc.vector.tensor_copy(out=a32[:], in_=inv_c_sb[:].rearrange("p g t -> p (g t)"))
-        nc.vector.tensor_tensor(
-            out=c32[:], in0=inv_c_sb[:].rearrange("p g t -> p (g t)"), in1=step_sb[:].rearrange("p g t -> p (g t)"), op=MULT
-        )
+        inv_c32 = sb.tile([P, 2 * PACK], F32, name="inv_c32")
+        gain32 = sb.tile([P, 2 * PACK], F32, name="gain32")
+        nc.vector.tensor_copy(out=inv_c32[:], in_=inv_c_sb)
+        nc.vector.tensor_tensor(out=gain32[:], in0=inv_c_sb, in1=step_sb, op=MULT)
         quantize_x(0, 3)
         for g in range(PASSES):
-            quantize_r(g)
-            quantize_r(PASSES + g)
+            quantize_r(0, g)
+            quantize_r(1, g)
         quantize_x(1, 0)
-        group_x_pool(1, 1, "xg_a")
-        group_x_pool(1, 2, "xg_b")
-        group_x_pool(1, 3, "xg_c")
+        group_x_gpsimd(1, 1, "x_grouped_a")
+        group_x_gpsimd(1, 2, "x_grouped_b")
+        group_x_gpsimd(1, 3, "x_grouped_c")
 
-        def qx(G, g):
-            quantize_x(G, g)
+        whole = {}
+        for n in range(STEPS - PACK):
+            unit, t = divmod(n, PACK)
+            if t == 0 and unit > 0:
+                group_y_gpsimd(unit - 1)
+            if t < 2 and n < LATE:
+                scale_r((PIECES_FIRST if unit == 0 else PIECES_NEXT)[t])
+            if t == 2 and unit == 0:
+                for g in range(1, PASSES):
+                    quantize_x(1, g)
+            if t == (3 if unit == 0 else 2) and n < LATE:
+                for g in range(PASSES):
+                    quantize_r(unit + 2, g)
+            if n >= HANDOVER:
+                empty_vector(n - EMPTY_LAG)
+            if t == 3 and unit > 0:
+                quantize_y(unit - 1, 0, CHUNK)
+            if t == 3 and unit < 2:
+                widen_vector(10 + unit)
+            if n == STEPS - PACK - 1:
+                store_scales(0, T - CHUNK, nc.sync)
+
+            if n in (1, 3):
+                weigh([(n, slice(0, CHUNK))], CHUNK, (widen, 8 + n // 2, 2))
+            elif EMPTY_LAG <= n < HANDOVER:
+                weigh([(n, slice(0, CHUNK))], CHUNK, (empty_y, n - EMPTY_LAG, nc.scalar.copy, 2))
+            else:
+                weigh([(n, slice(0, HALF)), (n, slice(HALF, CHUNK))], HALF, None)
+
+            if t == 0:
+                whole[unit] = sb.tile([P, PACK, CHUNK], F32, name="y", bufs=3)
+            finish(n, slice(0, CHUNK), whole[unit][:, t, :])
+            finished.add(n)
+            if t == 3:
+                for h in range(2):
+                    y[unit, h] = whole[unit][:, :, HALF * h : HALF * (h + 1)]
+                issue_y_turns()
             issue_products()
 
-        def qr(k0):
-            for k in range(k0, k0 + 4):
-                quantize_r(k)
-
-        def hv(n):
-            empty_y(n // 4, n % 4, None, "vector")
-
-        last = GROUPS * CHUNKS - 1
-
-        def weigh_pair(h, t0):
-            s = slice(HALF * h, HALF * (h + 1))
-            q, r, w = {}, {}, {}
+        def last_pair(h, t0):
+            cols = slice(HALF * h, HALF * (h + 1))
             if t0 == 0:
-                y[last, h] = sb.tile([P, PACK, HALF], F32, name="y", bufs=3)
-            for t in (t0, t0 + 1):
-                q[t] = sb.tile([P, HALF], F32, name="q", bufs=2)
-                nc.scalar.activation(out=q[t][:], in_=acc[4 * last + t][:, s], func=ACT.Square, scale=a32[:, 4 + t : 5 + t])
-            for t in (t0, t0 + 1):
-                r[t] = sb.tile([P, HALF], F32, name="r", bufs=2)
-                nc.scalar.activation(out=r[t][:], in_=q[t][:], func=ACT.Abs_reciprocal_sqrt, bias=1.0, scale=1.0)
-            for t in (t0, t0 + 1):
-                w[t] = sb.tile([P, HALF], F32, name="weight", bufs=4)
-                nc.scalar.activation(out=w[t][:], in_=r[t][:], func=ACT.Square)
-                nc.vector.scalar_tensor_tensor(
-                    out=y[last, h][:, t, :], in0=acc[4 * last + t][:, s], scalar=c32[:, 4 + t : 5 + t], in1=w[t][:], op0=MULT, op1=MULT
-                )
-            done.add(("y", 4 * last + t0 + 1, h))
-            issue_y_turns()
+                whole[LAST] = sb.tile([P, PACK, HALF], F32, name="y", bufs=3)
+            steps = (PACK * LAST + t0, PACK * LAST + t0 + 1)
+            weigh([(n, cols) for n in steps], HALF, None)
+            for n in steps:
+                finish(n, cols, whole[LAST][:, n % PACK, :])
+            if t0 == 2:
+                y[LAST, h] = whole[LAST][:]
+                issue_y_turns()
 
-        halves = {}
-
-        def planes_half(h):
-            s = slice(HALF * h, HALF * (h + 1))
-            grouped = sb.tile([P, HALF * PACK], BF16, name="y_grouped", bufs=1, align_bytes=64)
-            nc.vector.tensor_copy(
-                out=grouped[:].rearrange("p (a i t) -> p a t i", i=4, t=4),
-                in_=y[last, h][:].rearrange("p t (a i) -> p a t i", i=4),
-            )
-            halves[h] = grouped
-
-        def quantize_half(h):
-            cols = slice(T - CHUNK + HALF * h, T - CHUNK + HALF * (h + 1))
-            y_codes = sb.tile([P, HALF], U32, name="y_codes", bufs=2, align_bytes=64)
-            nc.vector.quantize_mx(out=y_codes[:].bitcast(E4X4), scales=y_scales[:, 1, cols], in_=halves[h][:])
-            nc.sync.dma_start(out=words_out[1][:, cols], in_=y_codes[:].bitcast(I32))
-
-        def hs(n):
-            empty_y(n // 4, n % 4, None, "scalar")
-
-        def ss(c0, c1):
-            store_scales(c0, c1, nc.sync if c0 == 0 else nc.scalar)
-
-        names = {"b": scale_r, "qx": qx, "qr": qr, "wv": widen_vector, "gy": group_y_pool, "qy": quantize_y, "hv": hv, "hs": hs,
-                 "ss": ss, "ph": planes_half, "qh": quantize_half, "gv": group_y}
-        supply, fills = PLAN
-        for n in range(STEPS + 1):
-            for item in supply[n]:
-                names[item[0]](*item[1:])
-            if n < STEPS - 4:
-                fill = None
-                if fills[n]:
-                    kind, j = fills[n]
-                    fill = widen_fill(j) if kind == "w" else empty_fill(j // 4, j % 4)
-                weigh(n, fill)
-                issue_turns()
-                finish(n)
-            elif n < STEPS:
-                weigh_pair((n % 4) // 2, 2 * (n % 2))
+        group_y_gpsimd(LAST - 1)
+        empty_vector(LATE - 1)
+        last_pair(0, 0)
+        empty_vector(LATE)
+        empty_vector(LATE + 1)
+        last_pair(0, 2)
+        quantize_y(LAST - 1, 0, CHUNK)
+        group_y_half(0)
+        empty_scalar(LATE + 2)
+        quantize_y(LAST, 0, HALF)
+        last_pair(1, 0)
+        empty_vector(LATE + 3)
+        last_pair(1, 2)
+        empty_scalar(STEPS - 4)
+        group_y_half(1)
+        empty_scalar(STEPS - 3)
+        quantize_y(LAST, HALF, CHUNK)
+        empty_scalar(STEPS - 2)
+        empty_vector(STEPS - 1)
+        store_scales(T - CHUNK, T, nc.scalar)

@@ -52,7 +52,7 @@ def tile_cauchy_influence_steps_b13_kernel(tc, R_bytes, R_scale, X, inv_c, step,
         r_raw, r_wide, spread, turned, r_scaled, r_codes, r_scales = {}, {}, {}, {}, {}, {}, {}
         x_raw, x_grouped, x_codes, x_scales = {}, {}, {}, {}
         acc, weight, y, y_turned, y_grouped, rows_out = {}, {}, {}, {}, {}, {}
-        widened, scaled, quantized, finished, emptied = set(), set(), set(), set(), set()
+        widened, scaled, quantized, finished = set(), set(), set(), set()
 
         warm = sb.tile([P, 1], F32, name="warm")
         nc.gpsimd.memset(warm[:], 1.0)
@@ -61,6 +61,20 @@ def tile_cauchy_influence_steps_b13_kernel(tc, R_bytes, R_scale, X, inv_c, step,
         ident = sb.tile([P, P], F32, name="ident")
         make_identity(nc, ident[:])
         y_scales = sb.tile([P, F // SPAN, T], U8, name="y_scales", align_bytes=64)
+
+        banks = {"acc_bank": ACC_BANKS, "turn_bank": TURN_BANKS, "out_bank": OUT_BANKS}
+        holders = {kind: [] for kind in banks}
+        left = set()
+
+        def free_bank(kinds):
+            for kind in kinds:
+                if len(holders[kind]) < banks[kind] or holders[kind][-banks[kind]] in left:
+                    return kind
+            return None
+
+        def take_bank(kind, holder, shape):
+            holders[kind].append(holder)
+            return ps.tile(shape, F32, name=kind, bufs=banks[kind])
 
         def load_bytes(i):
             r_raw[i] = sb.tile([P, K], U8, name="r_raw", bufs=10)
@@ -89,11 +103,12 @@ def tile_cauchy_influence_steps_b13_kernel(tc, R_bytes, R_scale, X, inv_c, step,
 
         def park_scales(raw, lo, hi, name):
             pairs = (hi - lo) // (2 * P)
-            bank = ps.tile([P, PACK, P], F32, name="out_bank", bufs=OUT_BANKS)
+            bank = take_bank("out_bank", name, [P, PACK, P])
             for j in range(pairs):
                 nc.tensor.transpose(bank[:, j, :], raw[:, j, :, :].rearrange("p h b -> p (h b)"), ident[:])
             rows = sb.tile([P, pairs, P], F32, name=name)
             nc.scalar.copy(out=rows[:], in_=bank[:, 0:pairs, :])
+            left.add(name)
             nc.scalar.dma_start(out=parked(lo, hi), in_=rows[:].rearrange("q j p -> q (j p)"))
 
         def load_spread(lo, hi, h, name):
@@ -144,9 +159,8 @@ def tile_cauchy_influence_steps_b13_kernel(tc, R_bytes, R_scale, X, inv_c, step,
         def issue_turns():
             for piece in range(len(turned), PIECES):
                 half, g = divmod(piece, PASSES)
-                free = piece < TURN_BANKS or piece - TURN_BANKS in scaled
-                if free and 2 * half + 1 in widened and len(turned) == piece:
-                    turned[piece] = ps.tile([P, 2, HALF], F32, name="turn_bank", bufs=TURN_BANKS)
+                if free_bank(("turn_bank",)) and 2 * half + 1 in widened and len(turned) == piece:
+                    turned[piece] = take_bank("turn_bank", ("r", piece), [P, 2, HALF])
                     for j in range(2):
                         words = r_wide[2 * half + j][:].bitcast(F32)
                         for u in range(2):
@@ -168,6 +182,7 @@ def tile_cauchy_influence_steps_b13_kernel(tc, R_bytes, R_scale, X, inv_c, step,
                     op=MULT,
                 )
                 scaled.add(piece)
+                left.add(("r", piece))
                 issue_turns()
 
         def quantize_r(half, g):
@@ -186,19 +201,11 @@ def tile_cauchy_influence_steps_b13_kernel(tc, R_bytes, R_scale, X, inv_c, step,
             for n in range(len(acc), STEPS):
                 unit, t = divmod(n, PACK)
                 chunk, G = divmod(unit, 2)
-                spare = n >= LATE and n % 2 == 1
-                if n < LATE:
-                    after = n - ACC_BANKS
-                elif spare:
-                    after = n - LATE_AHEAD
-                else:
-                    after = max(n - LATE_AHEAD, LATE - ACC_BANKS + (n - LATE) // 2)
                 ready = (2 * chunk + 1, PASSES - 1) in quantized and (G, PASSES - 1) in x_codes
-                if ready and (after < 0 or after in finished) and len(acc) == n:
-                    if spare:
-                        acc[n] = ps.tile([P, CHUNK], F32, name="turn_bank", bufs=TURN_BANKS)
-                    else:
-                        acc[n] = ps.tile([P, CHUNK], F32, name="acc_bank", bufs=ACC_BANKS)
+                due = n < LATE or len(finished) > n + 1 - n % 2 - LATE_AHEAD
+                kind = free_bank(("acc_bank",) if n < LATE else ("turn_bank", "acc_bank"))
+                if ready and due and kind and len(acc) == n:
+                    acc[n] = take_bank(kind, ("acc", n), [P, CHUNK])
                     cols = slice(P * t, P * (t + 1))
                     for g in range(PASSES):
                         nc.tensor.matmul_mx(
@@ -240,16 +247,9 @@ def tile_cauchy_influence_steps_b13_kernel(tc, R_bytes, R_scale, X, inv_c, step,
         def issue_y_turns():
             for j in range(len(y_turned), STEPS):
                 unit, i = divmod(j, PACK)
-                own_bank = j < LATE or i < OUT_BANKS
-                before = j - OUT_BANKS if j < LATE + OUT_BANKS else j - PACK
-                free = before < 0 or before in emptied or (not own_bank and unit < LAST)
-                if free and (unit, i // 2) in y and len(y_turned) == j:
-                    if own_bank:
-                        y_turned[j] = ps.tile([P, PACK, P], F32, name="out_bank", bufs=OUT_BANKS)
-                    elif i == 2:
-                        y_turned[j] = ps.tile([P, PACK, P], F32, name="acc_bank", bufs=ACC_BANKS)
-                    else:
-                        y_turned[j] = ps.tile([P, PACK, P], F32, name="turn_bank", bufs=TURN_BANKS)
+                kind = free_bank(("out_bank",) if j < LATE else ("out_bank", "acc_bank", "turn_bank"))
+                if kind and (unit, i // 2) in y and len(y_turned) == j:
+                    y_turned[j] = take_bank(kind, ("y", j), [P, PACK, P])
                     for t in range(PACK):
                         nc.tensor.transpose(y_turned[j][:, t, :], y[unit, i // 2][:, t, P * (i % 2) : P * (i % 2 + 1)], ident[:])
 
@@ -265,7 +265,7 @@ def tile_cauchy_influence_steps_b13_kernel(tc, R_bytes, R_scale, X, inv_c, step,
                 nc.sync.dma_start(
                     out=out_0[m0 : m0 + P, SPAN * G : SPAN * (G + 1)], in_=rows_out[j][:].rearrange("p m t -> p (m t)")
                 )
-                emptied.add(j)
+                left.add(("y", j))
                 issue_y_turns()
 
         def empty_vector(j):
@@ -359,7 +359,6 @@ def tile_cauchy_influence_steps_b13_kernel(tc, R_bytes, R_scale, X, inv_c, step,
         quantize_x(1, 0)
         group_x_gpsimd(1, 1, "x_grouped_a")
         group_x_gpsimd(1, 2, "x_grouped_b")
-        group_x_gpsimd(1, 3, "x_grouped_c")
 
         whole = {}
         for n in range(STEPS - PACK):
@@ -369,6 +368,7 @@ def tile_cauchy_influence_steps_b13_kernel(tc, R_bytes, R_scale, X, inv_c, step,
             if t < 2 and n < LATE:
                 scale_r((PIECES_FIRST if unit == 0 else PIECES_NEXT)[t])
             if t == 2 and unit == 0:
+                group_x(1, 3, "x_grouped_c")
                 for g in range(1, PASSES):
                     quantize_x(1, g)
             if t == (3 if unit == 0 else 2) and n < LATE:
@@ -378,13 +378,13 @@ def tile_cauchy_influence_steps_b13_kernel(tc, R_bytes, R_scale, X, inv_c, step,
                 empty_vector(n - EMPTY_LAG)
             if t == 3 and unit > 0:
                 quantize_y(unit - 1, 0, CHUNK)
-            if t == 3 and unit < 2:
-                widen_vector(10 + unit)
+            if n == 7:
+                widen_vector(11)
             if n == STEPS - PACK - 1:
                 store_scales(0, T - CHUNK, nc.sync)
 
-            if n in (1, 3):
-                weigh([(n, slice(0, CHUNK))], CHUNK, (widen, 8 + n // 2, 2))
+            if n < 3:
+                weigh([(n, slice(0, CHUNK))], CHUNK, (widen, 8 + n, 2))
             elif EMPTY_LAG <= n < HANDOVER:
                 weigh([(n, slice(0, CHUNK))], CHUNK, (empty_y, n - EMPTY_LAG, nc.scalar.copy, 2))
             else:
@@ -394,6 +394,7 @@ def tile_cauchy_influence_steps_b13_kernel(tc, R_bytes, R_scale, X, inv_c, step,
                 whole[unit] = sb.tile([P, PACK, CHUNK], F32, name="y", bufs=3)
             finish(n, slice(0, CHUNK), whole[unit][:, t, :])
             finished.add(n)
+            left.add(("acc", n))
             if t == 3:
                 for h in range(2):
                     y[unit, h] = whole[unit][:, :, HALF * h : HALF * (h + 1)]
@@ -408,6 +409,8 @@ def tile_cauchy_influence_steps_b13_kernel(tc, R_bytes, R_scale, X, inv_c, step,
             weigh([(n, cols) for n in steps], HALF, None)
             for n in steps:
                 finish(n, cols, whole[LAST][:, n % PACK, :])
+                if h == 1:
+                    left.add(("acc", n))
             if t0 == 2:
                 y[LAST, h] = whole[LAST][:]
                 issue_y_turns()
@@ -418,12 +421,12 @@ def tile_cauchy_influence_steps_b13_kernel(tc, R_bytes, R_scale, X, inv_c, step,
         empty_vector(LATE)
         empty_vector(LATE + 1)
         last_pair(0, 2)
+        empty_vector(LATE + 3)
+        empty_scalar(LATE + 2)
         quantize_y(LAST - 1, 0, CHUNK)
         group_y_half(0)
-        empty_scalar(LATE + 2)
-        quantize_y(LAST, 0, HALF)
         last_pair(1, 0)
-        empty_vector(LATE + 3)
+        quantize_y(LAST, 0, HALF)
         last_pair(1, 2)
         empty_scalar(STEPS - 4)
         group_y_half(1)

@@ -30,12 +30,10 @@ PIECES = (T // HALF) * PASSES
 LATE = STEPS - 2 * PACK
 LAST = UNITS - 1
 
-ACC_BANKS, TURN_BANKS, OUT_BANKS = 3, 3, 2
-
 PIECES_FIRST, PIECES_NEXT = (4, 3), (2, 1)
 EMPTY_LAG = 5
-HANDOVER = 14
-LATE_AHEAD = 5
+HEAD_STEPS = 3
+AHEAD, LATE_AHEAD = 4, 6
 
 
 def tile_cauchy_influence_steps_b13_kernel(tc, R_bytes, R_scale, X, inv_c, step, out_0, out_1, out_2):
@@ -51,30 +49,40 @@ def tile_cauchy_influence_steps_b13_kernel(tc, R_bytes, R_scale, X, inv_c, step,
 
         r_raw, r_wide, spread, turned, r_scaled, r_codes, r_scales = {}, {}, {}, {}, {}, {}, {}
         x_raw, x_grouped, x_codes, x_scales = {}, {}, {}, {}
-        acc, weight, y, y_turned, y_grouped, rows_out = {}, {}, {}, {}, {}, {}
+        acc, square, root, weight, y, y_turned, y_grouped = {}, {}, {}, {}, {}, {}, {}
         widened, scaled, quantized, finished = set(), set(), set(), set()
 
-        warm = sb.tile([P, 1], F32, name="warm")
-        nc.gpsimd.memset(warm[:], 1.0)
-        warm_out = sb.tile([P, 1], F32, name="warm_out")
-        nc.scalar.activation(out=warm_out[:], in_=warm[:], func=ACT.Abs_reciprocal_sqrt, bias=1.0, scale=1.0)
+        seed = sb.tile([P, 1], F32, name="seed")
+        nc.gpsimd.memset(seed[:], 1.0)
+        one_rounded = sb.tile([P, 1], F32, name="one_rounded")
+        nc.scalar.activation(out=one_rounded[:], in_=seed[:], func=ACT.Abs_reciprocal_sqrt)
+        one = sb.tile([P, 1], F32, name="one")
+        nc.scalar.activation(out=one[:], in_=one_rounded[:], func=ACT.Sign)
         ident = sb.tile([P, P], F32, name="ident")
         make_identity(nc, ident[:])
         y_scales = sb.tile([P, F // SPAN, T], U8, name="y_scales", align_bytes=64)
 
-        banks = {"acc_bank": ACC_BANKS, "turn_bank": TURN_BANKS, "out_bank": OUT_BANKS}
-        holders = {kind: [] for kind in banks}
-        left = set()
+        free = list(range(8))
+        held, bank_of = [], {}
 
-        def free_bank(kinds):
-            for kind in kinds:
-                if len(holders[kind]) < banks[kind] or holders[kind][-banks[kind]] in left:
-                    return kind
-            return None
+        def bank_free(kind):
+            if kind == "acc":
+                share = 6 if len(scaled) == PIECES else 3 if len(finished) < HEAD_STEPS else 4
+            elif kind == "r":
+                share = 3 if len(finished) < HEAD_STEPS else 2
+            else:
+                share = 2 if len(finished) < LATE else 4
+            return len(free) > 0 and len([holder for holder in held if holder[0] == kind]) < share
 
-        def take_bank(kind, holder, shape):
-            holders[kind].append(holder)
-            return ps.tile(shape, F32, name=kind, bufs=banks[kind])
+        def take_bank(holder, shape):
+            bank_of[holder] = free[0]
+            free.remove(bank_of[holder])
+            held.append(holder)
+            return ps.tile(shape, F32, name="bank%d" % bank_of[holder])
+
+        def leave_bank(holder):
+            held.remove(holder)
+            free.append(bank_of[holder])
 
         def load_bytes(i):
             r_raw[i] = sb.tile([P, K], U8, name="r_raw", bufs=10)
@@ -103,12 +111,12 @@ def tile_cauchy_influence_steps_b13_kernel(tc, R_bytes, R_scale, X, inv_c, step,
 
         def park_scales(raw, lo, hi, name):
             pairs = (hi - lo) // (2 * P)
-            bank = take_bank("out_bank", name, [P, PACK, P])
+            bank = take_bank(("y", name), [P, PACK, P])
             for j in range(pairs):
                 nc.tensor.transpose(bank[:, j, :], raw[:, j, :, :].rearrange("p h b -> p (h b)"), ident[:])
             rows = sb.tile([P, pairs, P], F32, name=name)
             nc.scalar.copy(out=rows[:], in_=bank[:, 0:pairs, :])
-            left.add(name)
+            leave_bank(("y", name))
             nc.scalar.dma_start(out=parked(lo, hi), in_=rows[:].rearrange("q j p -> q (j p)"))
 
         def load_spread(lo, hi, h, name):
@@ -141,26 +149,17 @@ def tile_cauchy_influence_steps_b13_kernel(tc, R_bytes, R_scale, X, inv_c, step,
             nc.vector.quantize_mx(out=x_codes[G, g][:].bitcast(E4X4), scales=x_scales[G, g][:], in_=x_grouped[G, g][:])
             issue_products()
 
-        def widen(i, parts, part):
-            if part == 0:
-                r_wide[i] = sb.tile([P, K], BF16, name="r_wide", bufs=8)
-            cols = slice(part * K // parts, (part + 1) * K // parts)
-            nc.scalar.copy(out=r_wide[i][:, cols], in_=r_raw[i][:, cols].bitcast(FP8))
-            if part == parts - 1:
-                widened.add(i)
-                issue_turns()
-
-        def widen_vector(i):
+        def widen(i, copy):
             r_wide[i] = sb.tile([P, K], BF16, name="r_wide", bufs=8)
-            nc.vector.tensor_copy(out=r_wide[i][:], in_=r_raw[i][:].bitcast(FP8))
+            copy(out=r_wide[i][:], in_=r_raw[i][:].bitcast(FP8))
             widened.add(i)
             issue_turns()
 
         def issue_turns():
             for piece in range(len(turned), PIECES):
                 half, g = divmod(piece, PASSES)
-                if free_bank(("turn_bank",)) and 2 * half + 1 in widened and len(turned) == piece:
-                    turned[piece] = take_bank("turn_bank", ("r", piece), [P, 2, HALF])
+                if bank_free("r") and 2 * half + 1 in widened and len(turned) == piece:
+                    turned[piece] = take_bank(("r", piece), [P, 2, HALF])
                     for j in range(2):
                         words = r_wide[2 * half + j][:].bitcast(F32)
                         for u in range(2):
@@ -182,7 +181,7 @@ def tile_cauchy_influence_steps_b13_kernel(tc, R_bytes, R_scale, X, inv_c, step,
                     op=MULT,
                 )
                 scaled.add(piece)
-                left.add(("r", piece))
+                leave_bank(("r", piece))
                 issue_turns()
 
         def quantize_r(half, g):
@@ -202,10 +201,9 @@ def tile_cauchy_influence_steps_b13_kernel(tc, R_bytes, R_scale, X, inv_c, step,
                 unit, t = divmod(n, PACK)
                 chunk, G = divmod(unit, 2)
                 ready = (2 * chunk + 1, PASSES - 1) in quantized and (G, PASSES - 1) in x_codes
-                due = n < LATE or len(finished) > n + 1 - n % 2 - LATE_AHEAD
-                kind = free_bank(("acc_bank",) if n < LATE else ("turn_bank", "acc_bank"))
-                if ready and due and kind and len(acc) == n:
-                    acc[n] = take_bank(kind, ("acc", n), [P, CHUNK])
+                due = n < PACK or len(finished) > n + n % 2 - (AHEAD if n < LATE else LATE_AHEAD)
+                if ready and due and bank_free("acc") and len(acc) == n:
+                    acc[n] = take_bank(("acc", n), [P, CHUNK])
                     cols = slice(P * t, P * (t + 1))
                     for g in range(PASSES):
                         nc.tensor.matmul_mx(
@@ -218,61 +216,46 @@ def tile_cauchy_influence_steps_b13_kernel(tc, R_bytes, R_scale, X, inv_c, step,
                             stop=(g == PASSES - 1),
                         )
 
-        def weigh(jobs, width, fill):
-            square, root = {}, {}
-            for n, cols in jobs:
-                square[n, cols.start] = sb.tile([P, width], F32, name="square", bufs=2)
-                nc.scalar.activation(
-                    out=square[n, cols.start][:], in_=acc[n][:, cols], func=ACT.Square, scale=inv_c32[:, n % 8 : n % 8 + 1]
-                )
-            if fill:
-                fill[0](*fill[1:], 0)
-            for n, cols in jobs:
-                root[n, cols.start] = sb.tile([P, width], F32, name="root", bufs=2)
-                nc.scalar.activation(
-                    out=root[n, cols.start][:], in_=square[n, cols.start][:], func=ACT.Abs_reciprocal_sqrt, bias=1.0, scale=1.0
-                )
-            if fill:
-                fill[0](*fill[1:], 1)
-            for n, cols in jobs:
-                if cols.start == 0 or n // PACK == LAST:
-                    weight[n] = sb.tile([P, CHUNK], F32, name="weight", bufs=4)
-                nc.scalar.activation(out=weight[n][:, cols], in_=root[n, cols.start][:], func=ACT.Square)
+        def square_scores(n, cols):
+            square[n] = sb.tile([P, cols.stop - cols.start], F32, name="square", bufs=2)
+            nc.scalar.activation(out=square[n][:], in_=acc[n][:, cols], func=ACT.Square, scale=inv_c32[:, n % 8 : n % 8 + 1])
+
+        def inverse_root(n):
+            root[n] = sb.tile(list(square[n].shape), F32, name="root", bufs=2)
+            nc.scalar.activation(out=root[n][:], in_=square[n][:], func=ACT.Abs_reciprocal_sqrt, bias=one[:])
+
+        def square_inverse_root(n):
+            weight[n] = sb.tile(list(root[n].shape), F32, name="weight", bufs=4)
+            nc.scalar.activation(out=weight[n][:], in_=root[n][:], func=ACT.Square)
 
         def finish(n, cols, result):
             nc.vector.scalar_tensor_tensor(
-                out=result, in0=acc[n][:, cols], scalar=gain32[:, n % 8 : n % 8 + 1], in1=weight[n][:, cols], op0=MULT, op1=MULT
+                out=result, in0=acc[n][:, cols], scalar=gain32[:, n % 8 : n % 8 + 1], in1=weight[n][:], op0=MULT, op1=MULT
             )
 
         def issue_y_turns():
             for j in range(len(y_turned), STEPS):
                 unit, i = divmod(j, PACK)
-                kind = free_bank(("out_bank",) if j < LATE else ("out_bank", "acc_bank", "turn_bank"))
-                if kind and (unit, i // 2) in y and len(y_turned) == j:
-                    y_turned[j] = take_bank(kind, ("y", j), [P, PACK, P])
+                if bank_free("y") and (unit, i // 2) in y and len(y_turned) == j:
+                    y_turned[j] = take_bank(("y", j), [P, PACK, P])
                     for t in range(PACK):
                         nc.tensor.transpose(y_turned[j][:, t, :], y[unit, i // 2][:, t, P * (i % 2) : P * (i % 2 + 1)], ident[:])
 
-        def empty_y(j, copy, parts, part):
+        def empty_y(j, copy):
             unit, i = divmod(j, PACK)
             chunk, G = divmod(unit, 2)
-            if part == 0:
-                rows_out[j] = sb.tile([P, P, PACK], F32, name="rows_out", bufs=6)
-            cols = slice(part * P // parts, (part + 1) * P // parts)
-            copy(out=rows_out[j][:, cols, :], in_=y_turned[j][:].rearrange("p t m -> p m t")[:, cols, :])
-            if part == parts - 1:
-                m0 = CHUNK * chunk + P * i
-                nc.sync.dma_start(
-                    out=out_0[m0 : m0 + P, SPAN * G : SPAN * (G + 1)], in_=rows_out[j][:].rearrange("p m t -> p (m t)")
-                )
-                left.add(("y", j))
-                issue_y_turns()
+            rows_out = sb.tile([P, P, PACK], F32, name="rows_out", bufs=6)
+            copy(out=rows_out[:], in_=y_turned[j][:].rearrange("p t m -> p m t"))
+            m0 = CHUNK * chunk + P * i
+            nc.sync.dma_start(out=out_0[m0 : m0 + P, SPAN * G : SPAN * (G + 1)], in_=rows_out[:].rearrange("p m t -> p (m t)"))
+            leave_bank(("y", j))
+            issue_y_turns()
 
         def empty_vector(j):
-            empty_y(j, nc.vector.tensor_copy, 1, 0)
+            empty_y(j, nc.vector.tensor_copy)
 
         def empty_scalar(j):
-            empty_y(j, nc.scalar.copy, 1, 0)
+            empty_y(j, nc.scalar.copy)
 
         def group_y_gpsimd(unit):
             y_grouped[unit] = sb.tile([P, CHUNK * PACK], BF16, name="y_grouped", align_bytes=64)
@@ -334,7 +317,7 @@ def tile_cauchy_influence_steps_b13_kernel(tc, R_bytes, R_scale, X, inv_c, step,
         step_sb = load_columns(step, "step_sb")
         load_bytes(7)
         for i in range(5):
-            widen(i, 1, 0)
+            widen(i, nc.scalar.copy)
         scale_r(2)
         park_scales(rest_scales, CHUNK, T, "scale_rows_rest")
         load_x(1, 2)
@@ -345,7 +328,7 @@ def tile_cauchy_influence_steps_b13_kernel(tc, R_bytes, R_scale, X, inv_c, step,
             load_bytes(i)
         load_spread(CHUNK, T, 1, "spread_rest")
         for i in range(5, 8):
-            widen(i, 1, 0)
+            widen(i, nc.scalar.copy)
         scale_r(2 * PASSES - 2)
 
         inv_c32 = sb.tile([P, 2 * PACK], F32, name="inv_c32")
@@ -361,7 +344,8 @@ def tile_cauchy_influence_steps_b13_kernel(tc, R_bytes, R_scale, X, inv_c, step,
         group_x_gpsimd(1, 2, "x_grouped_b")
 
         whole = {}
-        for n in range(STEPS - PACK):
+
+        def vector_step(n):
             unit, t = divmod(n, PACK)
             if t == 0 and unit > 0:
                 group_y_gpsimd(unit - 1)
@@ -374,43 +358,52 @@ def tile_cauchy_influence_steps_b13_kernel(tc, R_bytes, R_scale, X, inv_c, step,
             if t == (3 if unit == 0 else 2) and n < LATE:
                 for g in range(PASSES):
                     quantize_r(unit + 2, g)
-            if n >= HANDOVER:
+            if n >= LATE or (t == 3 and unit > 0):
                 empty_vector(n - EMPTY_LAG)
             if t == 3 and unit > 0:
                 quantize_y(unit - 1, 0, CHUNK)
-            if n == 7:
-                widen_vector(11)
+            if n == 2 * PACK - 1:
+                widen(T // P - 1, nc.vector.tensor_copy)
             if n == STEPS - PACK - 1:
                 store_scales(0, T - CHUNK, nc.sync)
-
-            if n < 3:
-                weigh([(n, slice(0, CHUNK))], CHUNK, (widen, 8 + n, 2))
-            elif EMPTY_LAG <= n < HANDOVER:
-                weigh([(n, slice(0, CHUNK))], CHUNK, (empty_y, n - EMPTY_LAG, nc.scalar.copy, 2))
-            else:
-                weigh([(n, slice(0, HALF)), (n, slice(HALF, CHUNK))], HALF, None)
-
             if t == 0:
                 whole[unit] = sb.tile([P, PACK, CHUNK], F32, name="y", bufs=3)
             finish(n, slice(0, CHUNK), whole[unit][:, t, :])
             finished.add(n)
-            left.add(("acc", n))
+            leave_bank(("acc", n))
             if t == 3:
                 for h in range(2):
                     y[unit, h] = whole[unit][:, :, HALF * h : HALF * (h + 1)]
                 issue_y_turns()
             issue_products()
 
+        for n in range(STEPS - PACK):
+            square_scores(n, slice(0, CHUNK))
+            if n > 0:
+                square_inverse_root(n - 1)
+                vector_step(n - 1)
+            inverse_root(n)
+            if n < 3:
+                widen(8 + n, nc.scalar.copy)
+            elif EMPTY_LAG <= n < LATE and n % PACK < 3:
+                empty_scalar(n - EMPTY_LAG)
+        square_inverse_root(STEPS - PACK - 1)
+        vector_step(STEPS - PACK - 1)
+
         def last_pair(h, t0):
             cols = slice(HALF * h, HALF * (h + 1))
             if t0 == 0:
                 whole[LAST] = sb.tile([P, PACK, HALF], F32, name="y", bufs=3)
             steps = (PACK * LAST + t0, PACK * LAST + t0 + 1)
-            weigh([(n, cols) for n in steps], HALF, None)
             for n in steps:
+                square_scores(n, cols)
+            for n in steps:
+                inverse_root(n)
+            for n in steps:
+                square_inverse_root(n)
                 finish(n, cols, whole[LAST][:, n % PACK, :])
                 if h == 1:
-                    left.add(("acc", n))
+                    leave_bank(("acc", n))
             if t0 == 2:
                 y[LAST, h] = whole[LAST][:]
                 issue_y_turns()
@@ -429,9 +422,9 @@ def tile_cauchy_influence_steps_b13_kernel(tc, R_bytes, R_scale, X, inv_c, step,
         quantize_y(LAST, 0, HALF)
         last_pair(1, 2)
         empty_scalar(STEPS - 4)
-        group_y_half(1)
         empty_scalar(STEPS - 3)
-        quantize_y(LAST, HALF, CHUNK)
+        group_y_half(1)
         empty_scalar(STEPS - 2)
         empty_vector(STEPS - 1)
+        quantize_y(LAST, HALF, CHUNK)
         store_scales(T - CHUNK, T, nc.scalar)

from contextlib import ExitStack

import concourse.mybir as mybir
from concourse.masks import make_identity

T, K, F = 1536, 2048, 1024
FLOPS = 2 * T * K * F

F32 = mybir.dt.float32
BF16 = mybir.dt.bfloat16
I32 = mybir.dt.int32
U32 = mybir.dt.uint32
U8 = mybir.dt.uint8
FP8 = mybir.dt.float8_e4m3fn
E4X4 = mybir.dt.float8_e4m3fn_x4
E5X4 = mybir.dt.float8_e5m2_x4
ACT = mybir.ActivationFunctionType
MULT = mybir.AluOpType.mult

P = 128
PACK = 4
SPAN = P * PACK
PASSES = K // SPAN
BLOCKS = K // 32
CHUNK = 512
HALF = CHUNK // 2
UNITS = (T // CHUNK) * (F // SPAN)
STEPS = PACK * UNITS
PIECES = (T // HALF) * PASSES
LATE = STEPS - 2 * PACK
LAST = UNITS - 1

PIECES_FIRST, PIECES_NEXT = (4, 3), (2, 1)
EMPTY_LAG = 5
HEAD_STEPS = 3
AHEAD, LATE_AHEAD = 4, 6


def tile_cauchy_influence_steps_b13_kernel(tc, R_bytes, R_scale, X, inv_c, step, out_0, out_1, out_2):
    nc = tc.nc
    with ExitStack() as ctx:
        sb = ctx.enter_context(tc.tile_pool(name="sb", bufs=1))
        ps = ctx.enter_context(tc.psum_pool(name="ps", bufs=1))
        ctx.enter_context(tc.manual_schedule())

        park = out_0[T - BLOCKS * T // F : T, :].rearrange("r n -> (r n)")
        words_out = out_1.rearrange("g p m t -> g p (m t)").bitcast(I32)
        scales_out = out_2.bitcast(I32)

        r_raw, r_wide, spread, turned, r_scaled, r_codes, r_scales = {}, {}, {}, {}, {}, {}, {}
        x_raw, x_grouped, x_codes, x_scales = {}, {}, {}, {}
        acc, square, root, weight, y, y_turned, y_grouped = {}, {}, {}, {}, {}, {}, {}
        widened, scaled, quantized, finished = set(), set(), set(), set()

        seed = sb.tile([P, 1], F32, name="seed")
        nc.gpsimd.memset(seed[:], 1.0)
        one_rounded = sb.tile([P, 1], F32, name="one_rounded")
        nc.scalar.activation(out=one_rounded[:], in_=seed[:], func=ACT.Abs_reciprocal_sqrt)
        one = sb.tile([P, 1], F32, name="one")
        nc.scalar.activation(out=one[:], in_=one_rounded[:], func=ACT.Sign)
        ident = sb.tile([P, P], F32, name="ident")
        make_identity(nc, ident[:])
        y_scales = sb.tile([P, F // SPAN, T], U8, name="y_scales", align_bytes=64)

        free = list(range(8))
        held, bank_of = [], {}

        def bank_free(kind):
            if kind == "acc":
                share = 6 if len(scaled) == PIECES else 3 if len(finished) < HEAD_STEPS else 4
            elif kind == "r":
                share = 3 if len(finished) < HEAD_STEPS else 2
            else:
                share = 2 if len(finished) < LATE else 4
            return len(free) > 0 and len([holder for holder in held if holder[0] == kind]) < share

        def take_bank(holder, shape):
            bank_of[holder] = free[0]
            free.remove(bank_of[holder])
            held.append(holder)
            return ps.tile(shape, F32, name="bank%d" % bank_of[holder])

        def leave_bank(holder):
            held.remove(holder)
            free.append(bank_of[holder])

        def load_bytes(i):
            r_raw[i] = sb.tile([P, K], U8, name="r_raw", bufs=10)
            nc.sync.dma_start(out=r_raw[i][:], in_=R_bytes[P * i : P * (i + 1), :])

        def load_x(G, g):
            x_raw[G, g] = sb.tile([P, PACK, SPAN], BF16, name="x_raw", bufs=5)
            rows = X[SPAN * g : SPAN * (g + 1), SPAN * G : SPAN * (G + 1)]
            nc.sync.dma_start(out=x_raw[G, g][:], in_=rows.rearrange("(p j) f -> p j f", j=PACK))

        def load_columns(vector, name):
            columns = sb.tile([P, F // SPAN, PACK], BF16, name=name)
            nc.sync.dma_start(out=columns[:], in_=vector.rearrange("o (g p t) -> p (o g) t", p=P, t=PACK))
            return columns[:].rearrange("p g t -> p (g t)")

        def load_scales(lo, hi, name):
            pairs = (hi - lo) // (2 * P)
            raw = sb.tile([P, pairs, 2, BLOCKS], F32, name=name)
            for h in range(2):
                rows = R_scale[lo + h * pairs * P : lo + (h + 1) * pairs * P, :]
                nc.sync.dma_start(out=raw[:, :, h, :], in_=rows.rearrange("(j p) b -> p j b", p=P))
            return raw

        def parked(lo, hi):
            return park[BLOCKS * lo : BLOCKS * hi].rearrange("(q m) -> q m", q=P)

        def park_scales(raw, lo, hi, name):
            pairs = (hi - lo) // (2 * P)
            bank = take_bank(("y", name), [P, PACK, P])
            for j in range(pairs):
                nc.tensor.transpose(bank[:, j, :], raw[:, j, :, :].rearrange("p h b -> p (h b)"), ident[:])
            rows = sb.tile([P, pairs, P], F32, name=name)
            nc.scalar.copy(out=rows[:], in_=bank[:, 0:pairs, :])
            leave_bank(("y", name))
            nc.scalar.dma_start(out=parked(lo, hi), in_=rows[:].rearrange("q j p -> q (j p)"))

        def load_spread(lo, hi, h, name):
            width = (hi - lo) // 2
            for g in range(PASSES):
                factors = sb.tile([P, width], F32, name=name, bufs=2 * PASSES)
                q0 = BLOCKS * h + 16 * g
                nc.sync.dma_start(out=factors[:], in_=parked(lo, hi)[q0 : q0 + 16, :].unsqueeze(1).to_broadcast([16, 8, width]))
                for m in range(0, width, HALF):
                    spread[(lo + h * width + m) // HALF, g] = factors[:, m : m + HALF]

        def group_x(G, g, name):
            x_grouped[G, g] = sb.tile([P, PACK * SPAN], BF16, name=name, align_bytes=64)
            nc.vector.tensor_copy(
                out=x_grouped[G, g][:].rearrange("p (t a e j) -> p a j e t", t=PACK, e=2, j=PACK),
                in_=x_raw[G, g][:].rearrange("p j (a e t) -> p a j e t", e=2, t=PACK),
            )

        def group_x_gpsimd(G, g, name):
            x_grouped[G, g] = sb.tile([P, PACK * SPAN], BF16, name=name, align_bytes=64)
            nc.gpsimd.tensor_scalar(
                out=x_grouped[G, g][:].rearrange("p (t m j) -> p t m j", t=PACK, j=PACK),
                in0=x_raw[G, g][:].rearrange("p j (m t) -> p t m j", t=PACK),
                scalar1=1.0, scalar2=1.0, op0=MULT, op1=MULT,
            )

        def quantize_x(G, g):
            x_codes[G, g] = sb.tile([P, SPAN], U32, name="x_codes", bufs=2 * PASSES, align_bytes=64)
            x_scales[G, g] = sb.tile([P, SPAN], U8, name="x_scales", bufs=2 * PASSES, align_bytes=64)
            nc.vector.quantize_mx(out=x_codes[G, g][:].bitcast(E4X4), scales=x_scales[G, g][:], in_=x_grouped[G, g][:])
            issue_products()

        def widen(i, copy):
            r_wide[i] = sb.tile([P, K], BF16, name="r_wide", bufs=8)
            copy(out=r_wide[i][:], in_=r_raw[i][:].bitcast(FP8))
            widened.add(i)
            issue_turns()

        def issue_turns():
            for piece in range(len(turned), PIECES):
                half, g = divmod(piece, PASSES)
                if bank_free("r") and 2 * half + 1 in widened and len(turned) == piece:
                    turned[piece] = take_bank(("r", piece), [P, 2, HALF])
                    for j in range(2):
                        words = r_wide[2 * half + j][:].bitcast(F32)
                        for u in range(2):
                            nc.tensor.transpose(
                                turned[piece][:, u, P * j : P * (j + 1)],
                                words[:, SPAN // 2 * g + u : SPAN // 2 * (g + 1) : 2],
                                ident[:],
                            )

        def scale_r(count):
            for piece in range(len(scaled), len(scaled) + count):
                half, g = divmod(piece, PASSES)
                r_scaled[piece] = sb.tile([P, HALF * PACK], BF16, name="r_scaled", bufs=2 * PASSES, align_bytes=64)
                values = turned[piece][:].rearrange("p u m -> p (u m)").bitcast(BF16)
                nc.vector.tensor_tensor(
                    out=r_scaled[piece][:].rearrange("p (m u e) -> p m u e", u=2, e=2),
                    in0=values.rearrange("p (u m e) -> p m u e", u=2, e=2),
                    in1=spread[half, g].unsqueeze(2).unsqueeze(3).to_broadcast([P, HALF, 2, 2]),
                    op=MULT,
                )
                scaled.add(piece)
                leave_bank(("r", piece))
                issue_turns()

        def quantize_r(half, g):
            chunk, h = divmod(half, 2)
            if h == 0:
                r_codes[chunk, g] = sb.tile([P, CHUNK], U32, name="r_codes", bufs=2 * PASSES, align_bytes=64)
                r_scales[chunk, g] = sb.tile([P, CHUNK], U8, name="r_scales", bufs=2 * PASSES, align_bytes=64)
            cols = slice(HALF * h, HALF * (h + 1))
            nc.vector.quantize_mx(
                out=r_codes[chunk, g][:, cols].bitcast(E5X4), scales=r_scales[chunk, g][:, cols], in_=r_scaled[PASSES * half + g][:]
            )
            quantized.add((half, g))
            issue_products()

        def issue_products():
            for n in range(len(acc), STEPS):
                unit, t = divmod(n, PACK)
                chunk, G = divmod(unit, 2)
                ready = (2 * chunk + 1, PASSES - 1) in quantized and (G, PASSES - 1) in x_codes
                due = n < PACK or len(finished) > n + n % 2 - (AHEAD if n < LATE else LATE_AHEAD)
                if ready and due and bank_free("acc") and len(acc) == n:
                    acc[n] = take_bank(("acc", n), [P, CHUNK])
                    cols = slice(P * t, P * (t + 1))
                    for g in range(PASSES):
                        nc.tensor.matmul_mx(
                            out=acc[n][:],
                            lhsT=x_codes[G, g][:, cols].bitcast(E4X4),
                            lhsT_scale=x_scales[G, g][:, cols],
                            rhs=r_codes[chunk, g][:].bitcast(E5X4),
                            rhs_scale=r_scales[chunk, g][:],
                            start=(g == 0),
                            stop=(g == PASSES - 1),
                        )

        def square_scores(n, cols):
            square[n] = sb.tile([P, cols.stop - cols.start], F32, name="square", bufs=2)
            nc.scalar.activation(out=square[n][:], in_=acc[n][:, cols], func=ACT.Square, scale=inv_c32[:, n % 8 : n % 8 + 1])

        def inverse_root(n):
            root[n] = sb.tile(list(square[n].shape), F32, name="root", bufs=2)
            nc.scalar.activation(out=root[n][:], in_=square[n][:], func=ACT.Abs_reciprocal_sqrt, bias=one[:])

        def square_inverse_root(n):
            weight[n] = sb.tile(list(root[n].shape), F32, name="weight", bufs=4)
            nc.scalar.activation(out=weight[n][:], in_=root[n][:], func=ACT.Square)

        def finish(n, cols, result):
            nc.vector.scalar_tensor_tensor(
                out=result, in0=acc[n][:, cols], scalar=gain32[:, n % 8 : n % 8 + 1], in1=weight[n][:], op0=MULT, op1=MULT
            )

        def issue_y_turns():
            for j in range(len(y_turned), STEPS):
                unit, i = divmod(j, PACK)
                if bank_free("y") and (unit, i // 2) in y and len(y_turned) == j:
                    y_turned[j] = take_bank(("y", j), [P, PACK, P])
                    for t in range(PACK):
                        nc.tensor.transpose(y_turned[j][:, t, :], y[unit, i // 2][:, t, P * (i % 2) : P * (i % 2 + 1)], ident[:])

        def empty_y(j, copy):
            unit, i = divmod(j, PACK)
            chunk, G = divmod(unit, 2)
            rows_out = sb.tile([P, P, PACK], F32, name="rows_out", bufs=6)
            copy(out=rows_out[:], in_=y_turned[j][:].rearrange("p t m -> p m t"))
            m0 = CHUNK * chunk + P * i
            nc.sync.dma_start(out=out_0[m0 : m0 + P, SPAN * G : SPAN * (G + 1)], in_=rows_out[:].rearrange("p m t -> p (m t)"))
            leave_bank(("y", j))
            issue_y_turns()

        def empty_vector(j):
            empty_y(j, nc.vector.tensor_copy)

        def empty_scalar(j):
            empty_y(j, nc.scalar.copy)

        def group_y_gpsimd(unit):
            y_grouped[unit] = sb.tile([P, CHUNK * PACK], BF16, name="y_grouped", align_bytes=64)
            nc.gpsimd.tensor_scalar(
                out=y_grouped[unit][:].rearrange("p (m t) -> p m t", t=PACK),
                in0=whole[unit][:].rearrange("p t m -> p m t"),
                scalar1=1.0, scalar2=1.0, op0=MULT, op1=MULT,
            )

        def group_y_half(h):
            y_grouped[LAST] = sb.tile([P, HALF * PACK], BF16, name="y_grouped", align_bytes=64)
            nc.vector.tensor_copy(
                out=y_grouped[LAST][:].rearrange("p (a i t) -> p a t i", i=4, t=PACK),
                in_=y[LAST, h].rearrange("p t (a i) -> p a t i", i=4),
            )

        def quantize_y(unit, lo, hi):
            chunk, G = divmod(unit, 2)
            cols = slice(CHUNK * chunk + lo, CHUNK * chunk + hi)
            y_codes = sb.tile([P, hi - lo], U32, name="y_codes", bufs=2, align_bytes=64)
            nc.vector.quantize_mx(out=y_codes[:].bitcast(E4X4), scales=y_scales[:, G, cols], in_=y_grouped[unit][:])
            nc.sync.dma_start(out=words_out[G][:, cols], in_=y_codes[:].bitcast(I32))

        def store_scales(lo, hi, queue):
            for Q in range(4):
                queue.dma_start(
                    out=scales_out[:, 4 * Q : 4 * Q + 4, lo // 4 : hi // 4].rearrange("g r m -> r g m"),
                    in_=y_scales[32 * Q : 32 * Q + 4, :, lo:hi].bitcast(I32),
                )

        load_x(0, 0)
        first_scales = load_scales(0, CHUNK, "scale_first")
        load_bytes(0)
        for g in (1, 2):
            load_x(0, g)
            load_bytes(g)
        park_scales(first_scales, 0, CHUNK, "scale_rows_first")
        load_x(0, 3)
        load_bytes(3)
        load_spread(0, CHUNK, 0, "spread_first")
        load_bytes(4)
        rest_scales = load_scales(CHUNK, T, "scale_rest")
        load_x(1, 0)
        load_spread(0, CHUNK, 1, "spread_first")

        group_x(0, 0, "x_grouped_a")
        group_x(0, 1, "x_grouped_b")
        quantize_x(0, 0)
        group_x(0, 2, "x_grouped_c")
        quantize_x(0, 1)
        quantize_x(0, 2)
        group_x_gpsimd(0, 3, "x_grouped_c")
        group_x_gpsimd(1, 0, "x_grouped_a")

        load_bytes(5)
        load_x(1, 1)
        load_bytes(6)
        inv_c_sb = load_columns(inv_c, "inv_c_sb")
        step_sb = load_columns(step, "step_sb")
        load_bytes(7)
        for i in range(5):
            widen(i, nc.scalar.copy)
        scale_r(2)
        park_scales(rest_scales, CHUNK, T, "scale_rows_rest")
        load_x(1, 2)
        load_spread(CHUNK, T, 0, "spread_rest")
        load_bytes(8)
        load_x(1, 3)
        for i in range(9, T // P):
            load_bytes(i)
        load_spread(CHUNK, T, 1, "spread_rest")
        for i in range(5, 8):
            widen(i, nc.scalar.copy)
        scale_r(2 * PASSES - 2)

        inv_c32 = sb.tile([P, 2 * PACK], F32, name="inv_c32")
        gain32 = sb.tile([P, 2 * PACK], F32, name="gain32")
        nc.vector.tensor_copy(out=inv_c32[:], in_=inv_c_sb)
        nc.vector.tensor_tensor(out=gain32[:], in0=inv_c_sb, in1=step_sb, op=MULT)
        quantize_x(0, 3)
        for g in range(PASSES):
            quantize_r(0, g)
            quantize_r(1, g)
        quantize_x(1, 0)
        group_x_gpsimd(1, 1, "x_grouped_a")
        group_x_gpsimd(1, 2, "x_grouped_b")

        whole = {}

        def vector_step(n):
            unit, t = divmod(n, PACK)
            if t == 0 and unit > 0:
                group_y_gpsimd(unit - 1)
            if t < 2 and n < LATE:
                scale_r((PIECES_FIRST if unit == 0 else PIECES_NEXT)[t])
            if t == 2 and unit == 0:
                group_x(1, 3, "x_grouped_c")
                for g in range(1, PASSES):
                    quantize_x(1, g)
            if t == (3 if unit == 0 else 2) and n < LATE:
                for g in range(PASSES):
                    quantize_r(unit + 2, g)
            if n >= LATE or (t == 3 and unit > 0):
                empty_vector(n - EMPTY_LAG)
            if t == 3 and unit > 0:
                quantize_y(unit - 1, 0, CHUNK)
            if n == 2 * PACK - 1:
                widen(T // P - 1, nc.vector.tensor_copy)
            if n == STEPS - PACK - 1:
                store_scales(0, T - CHUNK, nc.sync)
            if t == 0:
                whole[unit] = sb.tile([P, PACK, CHUNK], F32, name="y", bufs=3)
            finish(n, slice(0, CHUNK), whole[unit][:, t, :])
            finished.add(n)
            leave_bank(("acc", n))
            if t == 3:
                for h in range(2):
                    y[unit, h] = whole[unit][:, :, HALF * h : HALF * (h + 1)]
                issue_y_turns()
            issue_products()

        for n in range(STEPS - PACK):
            square_scores(n, slice(0, CHUNK))
            if n > 0:
                square_inverse_root(n - 1)
                vector_step(n - 1)
            inverse_root(n)
            if n < 3:
                widen(8 + n, nc.scalar.copy)
            elif EMPTY_LAG <= n < LATE and n % PACK < 3:
                empty_scalar(n - EMPTY_LAG)
        square_inverse_root(STEPS - PACK - 1)
        vector_step(STEPS - PACK - 1)

        def last_pair(h, t0):
            cols = slice(HALF * h, HALF * (h + 1))
            if t0 == 0:
                whole[LAST] = sb.tile([P, PACK, HALF], F32, name="y", bufs=3)
            steps = (PACK * LAST + t0, PACK * LAST + t0 + 1)
            for n in steps:
                square_scores(n, cols)
            for n in steps:
                inverse_root(n)
            for n in steps:
                square_inverse_root(n)
                finish(n, cols, whole[LAST][:, n % PACK, :])
                if h == 1:
                    leave_bank(("acc", n))
            if t0 == 2:
                y[LAST, h] = whole[LAST][:]
                issue_y_turns()

        group_y_gpsimd(LAST - 1)
        empty_vector(LATE - 1)
        last_pair(0, 0)
        empty_vector(LATE)
        empty_vector(LATE + 1)
        last_pair(0, 2)
        empty_vector(LATE + 3)
        empty_scalar(LATE + 2)
        quantize_y(LAST - 1, 0, CHUNK)
        group_y_half(0)
        last_pair(1, 0)
        quantize_y(LAST, 0, HALF)
        last_pair(1, 2)
        empty_scalar(STEPS - 4)
        empty_scalar(STEPS - 3)
        group_y_half(1)
        empty_scalar(STEPS - 2)
        empty_vector(STEPS - 1)
        quantize_y(LAST, HALF, CHUNK)
        store_scales(T - CHUNK, T, nc.scalar)
